import numpy as np
import ml_dtypes


def mxq(x, axis, fmt="e4m3"):
    dtype, down = {"e4m3": (ml_dtypes.float8_e4m3fn, 7), "e5m2": (ml_dtypes.float8_e5m2, 14)}[fmt]
    v = np.moveaxis(np.asarray(x, np.float32).astype(ml_dtypes.bfloat16).astype(np.float64), axis, -1)
    blocks = v.reshape(v.shape[:-1] + (-1, 32))
    amax = np.abs(blocks).max(-1, keepdims=True)
    byte = np.maximum(np.where(amax > 0, np.frexp(amax)[1] - 1 + 127, 0) - down, 1)
    scale = np.exp2(byte - 127.0)
    codes = (blocks / scale).astype(np.float32).astype(dtype).astype(np.float64)
    return np.moveaxis((codes * scale).reshape(v.shape), -1, axis)


WIDE = False


def mx_kscale(k):
    if not WIDE:
        return np.ones(k)
    levels = np.array([10, -10, 5, -5, 0])
    if k % 512:
        return np.exp2(np.random.permutation(np.resize(levels, k // 32))).repeat(32)
    a = np.empty((k // 512, 16))
    for p in range(k // 512):
        a[p, :8] = np.random.permutation(np.resize(levels, 8))
        for g in range(8):
            far = levels[np.abs(levels - a[p, g]) >= 10]
            a[p, g + 8] = far[np.random.randint(len(far))]
    return np.exp2(a.ravel()).repeat(32)


def f64(x):
    return np.asarray(x).astype(np.float64)


def striped(idx):
    return np.tile(np.asarray(idx).reshape(-1, 16).T, (8, 1)).astype(np.uint16)


def unstriped(offs):
    return offs[:16].T.reshape(-1).astype(np.int64)


E2M1 = np.array([0.0, 0.5, 1.0, 1.5, 2.0, 3.0, 4.0, 6.0, -0.0, -0.5, -1.0, -1.5, -2.0, -3.0, -4.0, -6.0])


def pack_weight(w, fmt):
    k, n = w.shape
    w = f64(np.asarray(w, np.float32).astype(ml_dtypes.bfloat16)).reshape(k // 32, 32, n)
    amax = np.abs(w).max(1)
    if fmt == "e4m3":
        byte = np.frexp(amax)[1] - 1 + 127 - 7
    else:
        mant, ex = np.frexp(amax / 6.0)
        byte = np.where(mant > 0.5, ex, ex - 1) + 127
    byte = np.clip(np.where(amax > 0, byte, 1), 1, 254)
    scaled = (w * np.exp2(127.0 - byte)[:, None, :]).reshape(k, n).astype(np.float32)
    by_word = np.ascontiguousarray(scaled.reshape(k // 512, 128, 4, n).transpose(0, 1, 3, 2))
    if fmt == "e4m3":
        words = by_word.astype(ml_dtypes.float8_e4m3fn).view(np.uint8)
    else:
        c = by_word.astype(ml_dtypes.float4_e2m1fn).view(np.uint8) & 0xF
        words = (c[..., 0::2] | (c[..., 1::2] << 4)).reshape(k // 512, 128, 2 * n)
    return np.ascontiguousarray(words), np.ascontiguousarray(byte.astype(np.uint8).reshape(k // 512, 16, n))


def unpack_weight(words, scales, fmt):
    g, _, n = scales.shape
    words = np.ascontiguousarray(words).reshape(g, 128, n, -1)
    if fmt == "e4m3":
        vals = words.view(ml_dtypes.float8_e4m3fn).astype(np.float64)
    else:
        nib = np.empty((g, 128, n, 4), np.uint8)
        nib[..., 0::2] = words & 0xF
        nib[..., 1::2] = words >> 4
        vals = E2M1[nib]
    vals = vals * np.repeat(np.exp2(scales.astype(np.float64) - 127.0), 8, axis=1)[..., None]
    return vals.transpose(0, 1, 3, 2).reshape(g * 512, n)


def gelu(v):
    return 0.5 * v * (1.0 + np.tanh(0.7978845608028654 * (v + 0.044715 * v ** 3)))


B, N, T, D, NQ = 1, 512, 2048, 1024, 512
DV = 512


def sgn(shape):
    return np.random.uniform(0.5, 2.0, shape) * np.where(np.random.standard_normal(shape) < 0, -1.0, 1.0)


def setup_inputs():
    n = np.random.standard_normal
    idx = np.sort(np.random.permutation(T)[:B * N].reshape(B, N), axis=1).reshape(-1)
    s = mx_kscale(D)[:, None]
    u = mx_kscale(N)
    ut = np.ones(T)
    ut[idx] = u
    kp = pack_weight(n((D, T)) / s, "e2m1")
    return {
        "qT": (n((B, D, NQ)) * s * (1.00 / np.sqrt(D))).astype(np.float32),
        "k_words": np.ascontiguousarray(kp[0].reshape(1, 2, 128, T, 2).transpose(0, 2, 3, 1, 4)).reshape(1, 128, T, 4),
        "k_scales": kp[1],
        "vT": (n((DV, T)) / ut).astype(np.float32),
        "us": (sgn((B, N, 1)) * u[:, None]).astype(np.float32),
        "offs": striped(idx),
    }


def reference(qT, k_words, k_scales, vT, us, offs):
    idx = unstriped(offs)
    pick = lambda x, which: x[:, which].reshape(x.shape[0], B, -1).transpose(1, 0, 2)
    k = unpack_weight(k_words.reshape(1, 128, T, 2, 2).transpose(0, 3, 1, 2, 4).reshape(2, 128, 2 * T), k_scales, "e2m1")
    kg = pick(k, idx)
    qq = mxq(f64(qT), 1, "e4m3")
    a = kg.transpose(0, 2, 1) @ qq
    y = gelu(a) * f64(us)
    wq = mxq(y, 1, "e4m3")
    o = wq.transpose(0, 2, 1) @ mxq(pick(f64(vT), idx).transpose(0, 2, 1), 1, "e4m3")
    return o

@@ -1,0 +1,170 @@
+from contextlib import ExitStack
+
+import concourse.mybir as mybir
+from concourse.masks import make_identity
+
+N, T, D, NQ, DV = 512, 2048, 1024, 512, 512
+FLOPS = 2 * N * D * NQ + 2 * NQ * N * DV
+
+F32 = mybir.dt.float32
+BF16 = mybir.dt.bfloat16
+I32 = mybir.dt.int32
+U32 = mybir.dt.uint32
+U16 = mybir.dt.uint16
+U8 = mybir.dt.uint8
+FP8X4 = mybir.dt.float8_e4m3fn_x4
+FP4X4 = mybir.dt.float4_e2m1fn_x4
+GELU = mybir.ActivationFunctionType.Gelu_apprx_tanh
+MULT = mybir.AluOpType.mult
+
+P = 128
+PACK = 4
+PASSES = D // (P * PACK)
+CHUNKS = NQ // P
+V_TILES = DV // P
+
+
+def interleave(copy, grouped, planes):
+    copy(
+        out=grouped.rearrange("p (c i) j -> p c j i", i=4),
+        in_=planes.rearrange("p j (c i) -> p c j i", i=4),
+    )
+
+
+def quantize(nc, pool, grouped, name):
+    width = grouped.shape[1]
+    codes = pool.tile([P, width], U32, name=name + "_codes", align_bytes=64)
+    scales = pool.tile([P, width], U8, name=name + "_scales", align_bytes=64)
+    nc.vector.quantize_mx(out=codes[:].bitcast(FP8X4), scales=scales[:], in_=grouped.rearrange("p w j -> p (w j)"))
+    return codes, scales
+
+
+def tile_attend_mlp_gelu_srt_kernel(tc, qT, k_words, k_scales, vT, us, offs, out):
+    nc = tc.nc
+    with ExitStack() as ctx:
+        sb = ctx.enter_context(tc.tile_pool(name="sb", bufs=1))
+        ps = ctx.enter_context(tc.psum_pool(name="ps", bufs=1))
+
+        offsets = sb.tile([P, N // 16], U16, name="offsets")
+        nc.sync.dma_start(offsets[:], offs)
+
+        scale_table = sb.tile([P, PASSES * T], U8, name="scale_table")
+        nc.vector.memset(scale_table[:].bitcast(I32), 0)
+
+        us_cols = sb.tile([P, PACK], F32, name="us_cols")
+        nc.gpsimd.dma_start(out=us_cols[:], in_=us[0].rearrange("(p t) x -> p (t x)", t=PACK))
+        ident = sb.tile([P, P], F32, name="ident")
+        make_identity(nc, ident[:])
+
+        q_raw = [sb.tile([P, PACK, NQ], F32, name="q_raw%d" % o) for o in range(PASSES)]
+        word_table = sb.tile([P, T], I32, name="word_table")
+        v_table = [sb.tile([P, T], F32, name="v_table%d" % j) for j in range(V_TILES)]
+
+        def load_q(o):
+            nc.sync.dma_start(out=q_raw[o][:], in_=qT[0, 512 * o : 512 * (o + 1), :].rearrange("(p j) w -> p j w", j=PACK))
+
+        load_q(0)
+        for quad in range(4):
+            nc.sync.dma_start(
+                out=scale_table[32 * quad : 32 * quad + 4, :].bitcast(I32).rearrange("f (o t) -> f o t", o=PASSES),
+                in_=k_scales[:, 4 * quad : 4 * quad + 4, :].bitcast(I32).rearrange("o f t -> f o t"),
+            )
+        nc.sync.dma_start(out=word_table[:], in_=k_words[0].rearrange("g t b -> g (t b)").bitcast(I32))
+        load_q(1)
+        for j in range(V_TILES):
+            nc.sync.dma_start(out=v_table[j][:], in_=vT[P * j : P * (j + 1), :])
+
+        q0_grouped = sb.tile([P, NQ, PACK], BF16, name="q0_grouped", align_bytes=64)
+        interleave(nc.scalar.copy, q0_grouped[:], q_raw[0][:])
+
+        scale_picked = sb.tile([P, PASSES, N], U8, name="scale_picked")
+        for o in range(PASSES):
+            nc.vector.tensor_copy(scale_picked[:, o, :], scale_table[:, o * T : (o + 1) * T].indirect(offsets[:]))
+        k_plane = sb.tile([P, PASSES, PACK, P], U8, name="k_plane", align_bytes=64)
+        nc.vector.tensor_copy(out=k_plane[:], in_=scale_picked[:].rearrange("p o (m t) -> p o t m", t=PACK))
+
+        word_picked = sb.tile([P, N], U32, name="word_picked")
+        nc.vector.tensor_copy(word_picked[:], word_table[:].bitcast(U32).indirect(offsets[:]))
+        k_codes = sb.tile([P, PASSES * PACK * P * 2], U8, name="k_codes", align_bytes=64)
+        nc.vector.tensor_copy(
+            out=k_codes[:].bitcast(U16).rearrange("p (t o m) -> p t m o", t=PACK, o=PASSES),
+            in_=word_picked[:].bitcast(U16).rearrange("p (m t o) -> p t m o", t=PACK, o=PASSES),
+        )
+
+        q0_codes, q0_scales = quantize(nc, sb, q0_grouped[:], "q0")
+
+        q1 = []
+        for c in range(CHUNKS):
+            grouped = sb.tile([P, P, PACK], BF16, name="q1_grouped%d" % c, align_bytes=64)
+            copy = nc.vector.tensor_copy if c < 2 else nc.scalar.copy
+            interleave(copy, grouped[:], q_raw[1][:, :, P * c : P * (c + 1)])
+            q1.append(grouped)
+        q1 = [quantize(nc, sb, q1[c][:], "q1_%d" % c) for c in range(CHUNKS)]
+
+        def first_layer(c):
+            cols = slice(P * c, P * (c + 1))
+            moving = [(q0_codes[:, cols], q0_scales[:, cols]), (q1[c][0][:], q1[c][1][:])]
+            acc = ps.tile([P, PACK, P], F32, name="acc", tag="acc", bufs=3)
+            for t in range(PACK):
+                for o in range(PASSES):
+                    at = (t * PASSES + o) * 2 * P
+                    nc.tensor.matmul_mx(
+                        out=acc[:, t, :],
+                        lhsT=k_codes[:, at : at + 2 * P].bitcast(FP4X4),
+                        lhsT_scale=k_plane[:, o, t, :],
+                        rhs=moving[o][0].bitcast(FP8X4),
+                        rhs_scale=moving[o][1],
+                        start=(o == 0),
+                        stop=(o == PASSES - 1),
+                    )
+            act = sb.tile([P, P, PACK], F32, name="act%d" % c)
+            nc.scalar.activation(out=act[:], in_=acc[:].rearrange("p t q -> p q t"), func=GELU)
+            y = sb.tile([P, P, PACK], BF16, name="y%d" % c, align_bytes=64)
+            nc.vector.tensor_tensor(out=y[:], in0=act[:], in1=us_cols[:].unsqueeze(1).to_broadcast([P, P, PACK]), op=MULT)
+            return quantize(nc, sb, y[:], "y%d" % c)
+
+        def values(j):
+            picked = sb.tile([P, N], BF16, name="v_picked%d" % j)
+            nc.vector.tensor_copy(picked[:], v_table[j][:].indirect(offsets[:]))
+            words = picked[:].bitcast(F32)
+            turned = ps.tile([P, 2, P], F32, name="turned", tag="turned", bufs=2)
+            for u in range(2):
+                nc.tensor.transpose(turned[:, u, :], words[:, u : 2 * P : 2], ident[:])
+            grouped = sb.tile([P, P, PACK], BF16, name="v_grouped%d" % j, align_bytes=64)
+            nc.scalar.copy(
+                out=grouped[:].rearrange("p e t -> p (e t)").bitcast(F32).rearrange("p (e u) -> p e u", u=2),
+                in_=turned[:].rearrange("p u e -> p e u"),
+            )
+            return quantize(nc, sb, grouped[:], "v%d" % j)
+
+        out_view = out[0].rearrange("(c p) e -> p c e", p=P)
+
+        def second_layer(j, v, ys, parts):
+            for cs, copy in parts:
+                acc = ps.tile([P, len(cs), P], F32, name="res", tag="res", bufs=3)
+                for i, c in enumerate(cs):
+                    nc.tensor.matmul_mx(
+                        out=acc[:, i, :],
+                        lhsT=ys[c][0][:].bitcast(FP8X4),
+                        lhsT_scale=ys[c][1][:],
+                        rhs=v[0][:].bitcast(FP8X4),
+                        rhs_scale=v[1][:],
+                        start=True,
+                        stop=True,
+                    )
+                res = sb.tile([P, len(cs), P], F32, name="res%d_%d" % (j, cs[0]))
+                copy(out=res[:], in_=acc[:])
+                nc.sync.dma_start(out=out_view[:, cs[0] : cs[-1] + 1, P * j : P * (j + 1)], in_=res[:])
+
+        ys, vs = [], []
+        ys.append(first_layer(0))
+        vs.append(values(0))
+        ys.append(first_layer(1))
+        ys.append(first_layer(2))
+        vs.append(values(1))
+        ys.append(first_layer(3))
+        vs.append(values(2))
+        for j in range(V_TILES - 1):
+            second_layer(j, vs[j], ys, [([0, 1, 2, 3], nc.scalar.copy)])
+        last = values(V_TILES - 1)
+        second_layer(V_TILES - 1, last, ys, [([0, 1], nc.scalar.copy), ([2, 3], nc.vector.tensor_copy)])

@@ -22,6 +22,7 @@ PACK = 4
 PASSES = D // (P * PACK)
 CHUNKS = NQ // P
 V_TILES = DV // P
+HALF = NQ // 2
 
 
 def interleave(copy, grouped, planes):
@@ -31,9 +32,9 @@ def interleave(copy, grouped, planes):
     )
 
 
-def quantize(nc, pool, grouped, name):
+def quantize(nc, pool, grouped, name, codes_tag=""):
     width = grouped.shape[1]
-    codes = pool.tile([P, width], U32, name=name + "_codes", align_bytes=64)
+    codes = pool.tile([P, width], U32, name=name + "_codes", tag=codes_tag, align_bytes=64)
     scales = pool.tile([P, width], U8, name=name + "_scales", align_bytes=64)
     nc.vector.quantize_mx(out=codes[:].bitcast(FP8X4), scales=scales[:], in_=grouped.rearrange("p w j -> p (w j)"))
     return codes, scales
@@ -48,7 +49,7 @@ def tile_attend_mlp_gelu_srt_kernel(tc, qT, k_words, k_scales, vT, us, offs, out
         offsets = sb.tile([P, N // 16], U16, name="offsets")
         nc.sync.dma_start(offsets[:], offs)
 
-        scale_table = sb.tile([P, PASSES * T], U8, name="scale_table")
+        scale_table = sb.tile([P, PASSES * T], U8, name="scale_table", tag="k_stage")
         nc.vector.memset(scale_table[:].bitcast(I32), 0)
 
         us_cols = sb.tile([P, PACK], F32, name="us_cols")
@@ -56,34 +57,45 @@ def tile_attend_mlp_gelu_srt_kernel(tc, qT, k_words, k_scales, vT, us, offs, out
         ident = sb.tile([P, P], F32, name="ident")
         make_identity(nc, ident[:])
 
-        q_raw = [sb.tile([P, PACK, NQ], F32, name="q_raw%d" % o) for o in range(PASSES)]
+        q_raw = {}
         word_table = sb.tile([P, T], I32, name="word_table")
-        v_table = [sb.tile([P, T], F32, name="v_table%d" % j) for j in range(V_TILES)]
+        v_table = [sb.tile([P, T], F32, name="v_table%d" % j, tag="v_stage%d" % j, align_bytes=64) for j in range(V_TILES)]
 
-        def load_q(o):
-            nc.sync.dma_start(out=q_raw[o][:], in_=qT[0, 512 * o : 512 * (o + 1), :].rearrange("(p j) w -> p j w", j=PACK))
+        def load_q(h, o):
+            q_raw[h, o] = sb.tile([P, PACK, HALF], F32, name="q_raw%d_%d" % (h, o), tag="q_stage%d_%d" % (h, o))
+            rows = qT[0, 512 * o : 512 * (o + 1), HALF * h : HALF * (h + 1)]
+            nc.sync.dma_start(out=q_raw[h, o][:], in_=rows.rearrange("(p j) w -> p j w", j=PACK))
 
-        load_q(0)
+        load_q(0, 0)
         for quad in range(4):
             nc.sync.dma_start(
                 out=scale_table[32 * quad : 32 * quad + 4, :].bitcast(I32).rearrange("f (o t) -> f o t", o=PASSES),
                 in_=k_scales[:, 4 * quad : 4 * quad + 4, :].bitcast(I32).rearrange("o f t -> f o t"),
             )
         nc.sync.dma_start(out=word_table[:], in_=k_words[0].rearrange("g t b -> g (t b)").bitcast(I32))
-        load_q(1)
+        load_q(0, 1)
+        load_q(1, 0)
+        load_q(1, 1)
         for j in range(V_TILES):
             nc.sync.dma_start(out=v_table[j][:], in_=vT[P * j : P * (j + 1), :])
 
-        q0_grouped = sb.tile([P, NQ, PACK], BF16, name="q0_grouped", align_bytes=64)
-        interleave(nc.scalar.copy, q0_grouped[:], q_raw[0][:])
+        warm = sb.tile([P, 2], F32, name="warm")
+        nc.vector.memset(warm[:, 0:1], 0.0)
+        nc.scalar.activation(out=warm[:, 1:2], in_=warm[:, 0:1], func=GELU)
 
-        scale_picked = sb.tile([P, PASSES, N], U8, name="scale_picked")
+        q_grouped = {}
+        for h in range(2):
+            for o in range(PASSES):
+                q_grouped[h, o] = sb.tile([P, HALF, PACK], BF16, name="q_grouped%d_%d" % (h, o), align_bytes=64)
+                interleave(nc.scalar.copy, q_grouped[h, o][:], q_raw[h, o][:])
+
+        scale_picked = sb.tile([P, PASSES, N], U8, name="scale_picked", tag="picked", align_bytes=64)
         for o in range(PASSES):
             nc.vector.tensor_copy(scale_picked[:, o, :], scale_table[:, o * T : (o + 1) * T].indirect(offsets[:]))
         k_plane = sb.tile([P, PASSES, PACK, P], U8, name="k_plane", align_bytes=64)
         nc.vector.tensor_copy(out=k_plane[:], in_=scale_picked[:].rearrange("p o (m t) -> p o t m", t=PACK))
 
-        word_picked = sb.tile([P, N], U32, name="word_picked")
+        word_picked = sb.tile([P, N], U32, name="word_picked", tag="k_stage")
         nc.vector.tensor_copy(word_picked[:], word_table[:].bitcast(U32).indirect(offsets[:]))
         k_codes = sb.tile([P, PASSES * PACK * P * 2], U8, name="k_codes", align_bytes=64)
         nc.vector.tensor_copy(
@@ -91,19 +103,16 @@ def tile_attend_mlp_gelu_srt_kernel(tc, qT, k_words, k_scales, vT, us, offs, out
             in_=word_picked[:].bitcast(U16).rearrange("p (m t o) -> p t m o", t=PACK, o=PASSES),
         )
 
-        q0_codes, q0_scales = quantize(nc, sb, q0_grouped[:], "q0")
+        q_mx = {}
+        for h in range(2):
+            for o in range(PASSES):
+                q_mx[h, o] = quantize(nc, sb, q_grouped[h, o][:], "q%d_%d" % (h, o), "picked" if h + o == 0 else "")
 
-        q1 = []
-        for c in range(CHUNKS):
-            grouped = sb.tile([P, P, PACK], BF16, name="q1_grouped%d" % c, align_bytes=64)
-            copy = nc.vector.tensor_copy if c < 2 else nc.scalar.copy
-            interleave(copy, grouped[:], q_raw[1][:, :, P * c : P * (c + 1)])
-            q1.append(grouped)
-        q1 = [quantize(nc, sb, q1[c][:], "q1_%d" % c) for c in range(CHUNKS)]
+        y, acts = {}, {}
 
         def first_layer(c):
-            cols = slice(P * c, P * (c + 1))
-            moving = [(q0_codes[:, cols], q0_scales[:, cols]), (q1[c][0][:], q1[c][1][:])]
+            cols = slice(P * (c % 2), P * (c % 2 + 1))
+            moving = [(q_mx[c // 2, o][0][:, cols], q_mx[c // 2, o][1][:, cols]) for o in range(PASSES)]
             acc = ps.tile([P, PACK, P], F32, name="acc", tag="acc", bufs=3)
             for t in range(PACK):
                 for o in range(PASSES):
@@ -117,54 +126,67 @@ def tile_attend_mlp_gelu_srt_kernel(tc, qT, k_words, k_scales, vT, us, offs, out
                         start=(o == 0),
                         stop=(o == PASSES - 1),
                     )
-            act = sb.tile([P, P, PACK], F32, name="act%d" % c)
-            nc.scalar.activation(out=act[:], in_=acc[:].rearrange("p t q -> p q t"), func=GELU)
-            y = sb.tile([P, P, PACK], BF16, name="y%d" % c, align_bytes=64)
-            nc.vector.tensor_tensor(out=y[:], in0=act[:], in1=us_cols[:].unsqueeze(1).to_broadcast([P, P, PACK]), op=MULT)
-            return quantize(nc, sb, y[:], "y%d" % c)
+            act = acts[c // 2][:, cols, :]
+            nc.scalar.activation(out=act, in_=acc[:].rearrange("p t q -> p q t"), func=GELU)
+            nc.vector.tensor_tensor(
+                out=y[c // 2][:, cols, :], in0=act, in1=us_cols[:].unsqueeze(1).to_broadcast([P, P, PACK]), op=MULT
+            )
 
-        def values(j):
+        def gather_values(j):
             picked = sb.tile([P, N], BF16, name="v_picked%d" % j)
             nc.vector.tensor_copy(picked[:], v_table[j][:].indirect(offsets[:]))
+            return picked
+
+        def turn_values(picked, grouped):
             words = picked[:].bitcast(F32)
             turned = ps.tile([P, 2, P], F32, name="turned", tag="turned", bufs=2)
             for u in range(2):
                 nc.tensor.transpose(turned[:, u, :], words[:, u : 2 * P : 2], ident[:])
-            grouped = sb.tile([P, P, PACK], BF16, name="v_grouped%d" % j, align_bytes=64)
             nc.scalar.copy(
-                out=grouped[:].rearrange("p e t -> p (e t)").bitcast(F32).rearrange("p (e u) -> p e u", u=2),
+                out=grouped.rearrange("p e t -> p (e t)").bitcast(F32).rearrange("p (e u) -> p e u", u=2),
                 in_=turned[:].rearrange("p u e -> p e u"),
             )
-            return quantize(nc, sb, grouped[:], "v%d" % j)
 
         out_view = out[0].rearrange("(c p) e -> p c e", p=P)
 
-        def second_layer(j, v, ys, parts):
-            for cs, copy in parts:
-                acc = ps.tile([P, len(cs), P], F32, name="res", tag="res", bufs=3)
-                for i, c in enumerate(cs):
-                    nc.tensor.matmul_mx(
-                        out=acc[:, i, :],
-                        lhsT=ys[c][0][:].bitcast(FP8X4),
-                        lhsT_scale=ys[c][1][:],
-                        rhs=v[0][:].bitcast(FP8X4),
-                        rhs_scale=v[1][:],
-                        start=True,
-                        stop=True,
-                    )
-                res = sb.tile([P, len(cs), P], F32, name="res%d_%d" % (j, cs[0]))
-                copy(out=res[:], in_=acc[:])
-                nc.sync.dma_start(out=out_view[:, cs[0] : cs[-1] + 1, P * j : P * (j + 1)], in_=res[:])
+        def second_layer(e0, v, chunks, copy):
+            width = v[0].shape[1]
+            acc = ps.tile([P, len(chunks), width], F32, name="res", tag="res", bufs=3)
+            for i, c in enumerate(chunks):
+                cols = slice(P * (c % 2), P * (c % 2 + 1))
+                nc.tensor.matmul_mx(
+                    out=acc[:, i, :],
+                    lhsT=y_mx[c // 2][0][:, cols].bitcast(FP8X4),
+                    lhsT_scale=y_mx[c // 2][1][:, cols],
+                    rhs=v[0][:].bitcast(FP8X4),
+                    rhs_scale=v[1][:],
+                    start=True,
+                    stop=True,
+                )
+            res = sb.tile([P, len(chunks), width], F32, name="res%d_%d" % (e0, chunks[0]))
+            copy(out=res[:], in_=acc[:])
+            nc.sync.dma_start(out=out_view[:, chunks[0] : chunks[-1] + 1, e0 : e0 + width], in_=res[:])
 
-        ys, vs = [], []
-        ys.append(first_layer(0))
-        vs.append(values(0))
-        ys.append(first_layer(1))
-        ys.append(first_layer(2))
-        vs.append(values(1))
-        ys.append(first_layer(3))
-        vs.append(values(2))
-        for j in range(V_TILES - 1):
-            second_layer(j, vs[j], ys, [([0, 1, 2, 3], nc.scalar.copy)])
-        last = values(V_TILES - 1)
-        second_layer(V_TILES - 1, last, ys, [([0, 1], nc.scalar.copy), ([2, 3], nc.vector.tensor_copy)])
+        y_mx = []
+        v01 = sb.tile([P, 2 * P, PACK], BF16, name="v01", align_bytes=64)
+        for h in range(2):
+            picked = gather_values(h)
+            y[h] = sb.tile([P, HALF, PACK], BF16, name="y%d" % h, tag="v_stage%d" % h, align_bytes=64)
+            acts[h] = sb.tile([P, HALF, PACK], F32, name="act%d" % h, tag="q_stage1_%d" % (1 - h))
+            first_layer(2 * h)
+            first_layer(2 * h + 1)
+            y_mx.append(quantize(nc, sb, y[h][:], "y%d" % h))
+            turn_values(picked, v01[:, P * h : P * (h + 1), :])
+        v01_mx = quantize(nc, sb, v01[:], "v01", "v_stage1")
+        picked = [gather_values(j) for j in (2, 3)]
+        second_layer(0, v01_mx, [0, 1], nc.scalar.copy)
+        second_layer(0, v01_mx, [2, 3], nc.scalar.copy)
+        v2 = sb.tile([P, P, PACK], BF16, name="v2", align_bytes=64)
+        v3 = sb.tile([P, P, PACK], BF16, name="v3", align_bytes=64)
+        turn_values(picked[0], v2[:])
+        turn_values(picked[1], v3[:])
+        v2_mx = quantize(nc, sb, v2[:], "v2", "v_stage3")
+        v3_mx = quantize(nc, sb, v3[:], "v3")
+        second_layer(2 * P, v2_mx, [0, 1, 2, 3], nc.scalar.copy)
+        second_layer(3 * P, v3_mx, [0, 1], nc.vector.tensor_copy)
+        second_layer(3 * P, v3_mx, [2, 3], nc.scalar.copy)

@@ -49,53 +49,47 @@ def tile_attend_mlp_gelu_srt_kernel(tc, qT, k_words, k_scales, vT, us, offs, out
         offsets = sb.tile([P, N // 16], U16, name="offsets")
         nc.sync.dma_start(offsets[:], offs)
 
-        scale_table = sb.tile([P, PASSES * T], U8, name="scale_table", tag="k_stage")
-        nc.vector.memset(scale_table[:].bitcast(I32), 0)
+        scale_table = sb.tile([P, T], U8, name="scale_table")
+        nc.sync.dma_start(out=scale_table[0:32, :].bitcast(I32), in_=k_scales.rearrange("o f t -> (o f) t").bitcast(I32))
+        nc.vector.memset(scale_table[32:64, :].bitcast(I32), 0)
+        nc.vector.memset(scale_table[64:128, :].bitcast(I32), 0)
+        k_plane = [sb.tile([P, PACK * P], U8, name="k_plane%d" % o, align_bytes=64) for o in range(PASSES)]
+        nc.vector.memset(k_plane[1][:].bitcast(I32), 0)
 
         us_cols = sb.tile([P, PACK], F32, name="us_cols")
         nc.gpsimd.dma_start(out=us_cols[:], in_=us[0].rearrange("(p t) x -> p (t x)", t=PACK))
         ident = sb.tile([P, P], F32, name="ident")
         make_identity(nc, ident[:])
 
-        q_raw = {}
-        word_table = sb.tile([P, T], I32, name="word_table")
-        v_table = [sb.tile([P, T], F32, name="v_table%d" % j, tag="v_stage%d" % j, align_bytes=64) for j in range(V_TILES)]
-
-        def load_q(h, o):
-            q_raw[h, o] = sb.tile([P, PACK, HALF], F32, name="q_raw%d_%d" % (h, o), tag="q_stage%d_%d" % (h, o))
-            rows = qT[0, 512 * o : 512 * (o + 1), HALF * h : HALF * (h + 1)]
-            nc.sync.dma_start(out=q_raw[h, o][:], in_=rows.rearrange("(p j) w -> p j w", j=PACK))
-
-        load_q(0, 0)
-        for quad in range(4):
-            nc.sync.dma_start(
-                out=scale_table[32 * quad : 32 * quad + 4, :].bitcast(I32).rearrange("f (o t) -> f o t", o=PASSES),
-                in_=k_scales[:, 4 * quad : 4 * quad + 4, :].bitcast(I32).rearrange("o f t -> f o t"),
-            )
+        word_table = sb.tile([P, T], I32, name="word_table", tag="stage0", align_bytes=64)
         nc.sync.dma_start(out=word_table[:], in_=k_words[0].rearrange("g t b -> g (t b)").bitcast(I32))
-        load_q(0, 1)
-        load_q(1, 0)
-        load_q(1, 1)
-        for j in range(V_TILES):
-            nc.sync.dma_start(out=v_table[j][:], in_=vT[P * j : P * (j + 1), :])
+        q_rows = [qT[0, 512 * o : 512 * (o + 1), :].rearrange("(p j) w -> p j w", j=PACK) for o in range(PASSES)]
+        q0_raw = sb.tile([P, PACK, NQ], F32, name="q0_raw", tag="stage2", align_bytes=64)
+        nc.sync.dma_start(out=q0_raw[:], in_=q_rows[0])
+        q_raw = {(h, 0): q0_raw[:, :, HALF * h : HALF * (h + 1)] for h in range(2)}
+        for h, tag in enumerate(["stage3", "stage4"]):
+            q1_raw = sb.tile([P, PACK, HALF], F32, name="q1_raw%d" % h, tag=tag, align_bytes=64)
+            nc.sync.dma_start(out=q1_raw[:], in_=q_rows[1][:, :, HALF * h : HALF * (h + 1)])
+            q_raw[h, 1] = q1_raw[:]
 
         warm = sb.tile([P, 2], F32, name="warm")
         nc.vector.memset(warm[:, 0:1], 0.0)
         nc.scalar.activation(out=warm[:, 1:2], in_=warm[:, 0:1], func=GELU)
 
-        q_grouped = {}
-        for h in range(2):
-            for o in range(PASSES):
-                q_grouped[h, o] = sb.tile([P, HALF, PACK], BF16, name="q_grouped%d_%d" % (h, o), align_bytes=64)
-                interleave(nc.scalar.copy, q_grouped[h, o][:], q_raw[h, o][:])
+        scale_picked = sb.tile([P, N], U8, name="scale_picked")
+        nc.vector.tensor_copy(scale_picked[:], scale_table[:].indirect(offsets[:]))
+        nc.vector.tensor_copy(
+            out=k_plane[0][:].rearrange("p (t m) -> p t m", t=PACK), in_=scale_picked[:].rearrange("p (m t) -> p t m", t=PACK)
+        )
+        moves = [(o, quad) for o in range(PASSES) for quad in range(4) if o + quad > 0]
+        for i, (o, quad) in enumerate(moves):
+            queue = nc.scalar if i < 5 else nc.gpsimd
+            row = 16 * o + 4 * quad
+            queue.dma_start(
+                out=k_plane[o][32 * quad : 32 * quad + 4, :].bitcast(I32), in_=k_plane[0][row : row + 4, :].bitcast(I32)
+            )
 
-        scale_picked = sb.tile([P, PASSES, N], U8, name="scale_picked", tag="picked", align_bytes=64)
-        for o in range(PASSES):
-            nc.vector.tensor_copy(scale_picked[:, o, :], scale_table[:, o * T : (o + 1) * T].indirect(offsets[:]))
-        k_plane = sb.tile([P, PASSES, PACK, P], U8, name="k_plane", align_bytes=64)
-        nc.vector.tensor_copy(out=k_plane[:], in_=scale_picked[:].rearrange("p o (m t) -> p o t m", t=PACK))
-
-        word_picked = sb.tile([P, N], U32, name="word_picked", tag="k_stage")
+        word_picked = sb.tile([P, N], U32, name="word_picked", tag="stage1", align_bytes=64)
         nc.vector.tensor_copy(word_picked[:], word_table[:].bitcast(U32).indirect(offsets[:]))
         k_codes = sb.tile([P, PASSES * PACK * P * 2], U8, name="k_codes", align_bytes=64)
         nc.vector.tensor_copy(
@@ -104,9 +98,16 @@ def tile_attend_mlp_gelu_srt_kernel(tc, qT, k_words, k_scales, vT, us, offs, out
         )
 
         q_mx = {}
-        for h in range(2):
+        for h, copy in enumerate([nc.vector.tensor_copy, nc.scalar.copy]):
             for o in range(PASSES):
-                q_mx[h, o] = quantize(nc, sb, q_grouped[h, o][:], "q%d_%d" % (h, o), "picked" if h + o == 0 else "")
+                grouped = sb.tile([P, HALF, PACK], BF16, name="q_grouped%d_%d" % (h, o), align_bytes=64)
+                interleave(copy, grouped[:], q_raw[h, o])
+                q_mx[h, o] = quantize(nc, sb, grouped[:], "q%d_%d" % (h, o))
+
+        v_table = []
+        for j in range(V_TILES):
+            v_table.append(sb.tile([P, T], F32, name="v_table%d" % j, tag="stage%d" % j, align_bytes=64))
+            nc.sync.dma_start(out=v_table[j][:], in_=vT[P * j : P * (j + 1), :])
 
         y, acts = {}, {}
 
@@ -120,7 +121,7 @@ def tile_attend_mlp_gelu_srt_kernel(tc, qT, k_words, k_scales, vT, us, offs, out
                     nc.tensor.matmul_mx(
                         out=acc[:, t, :],
                         lhsT=k_codes[:, at : at + 2 * P].bitcast(FP4X4),
-                        lhsT_scale=k_plane[:, o, t, :],
+                        lhsT_scale=k_plane[o][:, P * t : P * (t + 1)],
                         rhs=moving[o][0].bitcast(FP8X4),
                         rhs_scale=moving[o][1],
                         start=(o == 0),
@@ -171,13 +172,13 @@ def tile_attend_mlp_gelu_srt_kernel(tc, qT, k_words, k_scales, vT, us, offs, out
         v01 = sb.tile([P, 2 * P, PACK], BF16, name="v01", align_bytes=64)
         for h in range(2):
             picked = gather_values(h)
-            y[h] = sb.tile([P, HALF, PACK], BF16, name="y%d" % h, tag="v_stage%d" % h, align_bytes=64)
-            acts[h] = sb.tile([P, HALF, PACK], F32, name="act%d" % h, tag="q_stage1_%d" % (1 - h))
+            y[h] = sb.tile([P, HALF, PACK], BF16, name="y%d" % h, tag="stage%d" % h, align_bytes=64)
+            acts[h] = sb.tile([P, HALF, PACK], F32, name="act%d" % h, tag=["stage4", "act1"][h], align_bytes=64)
             first_layer(2 * h)
             first_layer(2 * h + 1)
             y_mx.append(quantize(nc, sb, y[h][:], "y%d" % h))
             turn_values(picked, v01[:, P * h : P * (h + 1), :])
-        v01_mx = quantize(nc, sb, v01[:], "v01", "v_stage1")
+        v01_mx = quantize(nc, sb, v01[:], "v01", "stage1")
         picked = [gather_values(j) for j in (2, 3)]
         second_layer(0, v01_mx, [0, 1], nc.scalar.copy)
         second_layer(0, v01_mx, [2, 3], nc.scalar.copy)
@@ -185,7 +186,7 @@ def tile_attend_mlp_gelu_srt_kernel(tc, qT, k_words, k_scales, vT, us, offs, out
         v3 = sb.tile([P, P, PACK], BF16, name="v3", align_bytes=64)
         turn_values(picked[0], v2[:])
         turn_values(picked[1], v3[:])
-        v2_mx = quantize(nc, sb, v2[:], "v2", "v_stage3")
+        v2_mx = quantize(nc, sb, v2[:], "v2", "stage3")
         v3_mx = quantize(nc, sb, v3[:], "v3")
         second_layer(2 * P, v2_mx, [0, 1, 2, 3], nc.scalar.copy)
         second_layer(3 * P, v3_mx, [0, 1], nc.vector.tensor_copy)

@@ -26,10 +26,7 @@ HALF = NQ // 2
 
 
 def interleave(copy, grouped, planes):
-    copy(
-        out=grouped.rearrange("p (c i) j -> p c j i", i=4),
-        in_=planes.rearrange("p j (c i) -> p c j i", i=4),
-    )
+    copy(out=grouped, in_=planes.rearrange("p j w -> p w j"))
 
 
 def quantize(nc, pool, grouped, name, codes_tag=""):
@@ -83,7 +80,7 @@ def tile_attend_mlp_gelu_srt_kernel(tc, qT, k_words, k_scales, vT, us, offs, out
         )
         moves = [(o, quad) for o in range(PASSES) for quad in range(4) if o + quad > 0]
         for i, (o, quad) in enumerate(moves):
-            queue = nc.scalar if i < 5 else nc.gpsimd
+            queue = nc.scalar if i < 6 else nc.gpsimd
             row = 16 * o + 4 * quad
             queue.dma_start(
                 out=k_plane[o][32 * quad : 32 * quad + 4, :].bitcast(I32), in_=k_plane[0][row : row + 4, :].bitcast(I32)

@@ -19,21 +19,27 @@ MULT = mybir.AluOpType.mult
 
 P = 128
 PACK = 4
-PASSES = D // (P * PACK)
-CHUNKS = NQ // P
+K_PASS = P * PACK
+PASSES = D // K_PASS
+QUADS = 4
 V_TILES = DV // P
 HALF = NQ // 2
+BUFFER = 4 * T
+MOVES_ON_SCALAR = 5
+LAYER_BANKS = 3
+RESULT_BANKS = 5
 
 
 def interleave(copy, grouped, planes):
-    copy(out=grouped, in_=planes.rearrange("p j w -> p w j"))
+    copy(out=grouped, in_=planes.rearrange("p t w -> p w t"))
 
 
-def quantize(nc, pool, grouped, name, codes_tag=""):
+def quantize(nc, pool, grouped, name, codes=None):
     width = grouped.shape[1]
-    codes = pool.tile([P, width], U32, name=name + "_codes", tag=codes_tag, align_bytes=64)
+    if codes is None:
+        codes = pool.tile([P, width], U32, name=name + "_codes", align_bytes=64)
     scales = pool.tile([P, width], U8, name=name + "_scales", align_bytes=64)
-    nc.vector.quantize_mx(out=codes[:].bitcast(FP8X4), scales=scales[:], in_=grouped.rearrange("p w j -> p (w j)"))
+    nc.vector.quantize_mx(out=codes[:].bitcast(FP8X4), scales=scales[:], in_=grouped.rearrange("p w t -> p (w t)"))
     return codes, scales
 
 
@@ -41,7 +47,11 @@ def tile_attend_mlp_gelu_srt_kernel(tc, qT, k_words, k_scales, vT, us, offs, out
     nc = tc.nc
     with ExitStack() as ctx:
         sb = ctx.enter_context(tc.tile_pool(name="sb", bufs=1))
+        staging = ctx.enter_context(tc.tile_pool(name="staging", bufs=1))
         ps = ctx.enter_context(tc.psum_pool(name="ps", bufs=1))
+
+        def staged(shape, dtype, name, buffer, at=0):
+            return staging.tile(shape, dtype, name=name, offset=buffer * BUFFER + at, align_bytes=64)
 
         offsets = sb.tile([P, N // 16], U16, name="offsets")
         nc.sync.dma_start(offsets[:], offs)
@@ -58,14 +68,14 @@ def tile_attend_mlp_gelu_srt_kernel(tc, qT, k_words, k_scales, vT, us, offs, out
         ident = sb.tile([P, P], F32, name="ident")
         make_identity(nc, ident[:])
 
-        word_table = sb.tile([P, T], I32, name="word_table", tag="stage0", align_bytes=64)
+        word_table = staged([P, T], I32, "word_table", 0)
         nc.sync.dma_start(out=word_table[:], in_=k_words[0].rearrange("g t b -> g (t b)").bitcast(I32))
-        q_rows = [qT[0, 512 * o : 512 * (o + 1), :].rearrange("(p j) w -> p j w", j=PACK) for o in range(PASSES)]
-        q0_raw = sb.tile([P, PACK, NQ], F32, name="q0_raw", tag="stage2", align_bytes=64)
+        q_rows = [qT[0, K_PASS * o : K_PASS * (o + 1), :].rearrange("(p t) w -> p t w", t=PACK) for o in range(PASSES)]
+        q0_raw = staged([P, PACK, NQ], F32, "q0_raw", 2)
         nc.sync.dma_start(out=q0_raw[:], in_=q_rows[0])
         q_raw = {(h, 0): q0_raw[:, :, HALF * h : HALF * (h + 1)] for h in range(2)}
-        for h, tag in enumerate(["stage3", "stage4"]):
-            q1_raw = sb.tile([P, PACK, HALF], F32, name="q1_raw%d" % h, tag=tag, align_bytes=64)
+        for h in range(2):
+            q1_raw = staged([P, PACK, HALF], F32, "q1_raw%d" % h, 3 + h)
             nc.sync.dma_start(out=q1_raw[:], in_=q_rows[1][:, :, HALF * h : HALF * (h + 1)])
             q_raw[h, 1] = q1_raw[:]
 
@@ -78,15 +88,15 @@ def tile_attend_mlp_gelu_srt_kernel(tc, qT, k_words, k_scales, vT, us, offs, out
         nc.vector.tensor_copy(
             out=k_plane[0][:].rearrange("p (t m) -> p t m", t=PACK), in_=scale_picked[:].rearrange("p (m t) -> p t m", t=PACK)
         )
-        moves = [(o, quad) for o in range(PASSES) for quad in range(4) if o + quad > 0]
-        for i, (o, quad) in enumerate(moves):
-            queue = nc.scalar if i < 6 else nc.gpsimd
+        moves = [(o, quad) for o in range(PASSES) for quad in range(QUADS) if (o, quad) != (0, 0)]
+        for number, (o, quad) in enumerate(moves):
+            queue = nc.scalar if number < MOVES_ON_SCALAR else nc.gpsimd
             row = 16 * o + 4 * quad
             queue.dma_start(
                 out=k_plane[o][32 * quad : 32 * quad + 4, :].bitcast(I32), in_=k_plane[0][row : row + 4, :].bitcast(I32)
             )
 
-        word_picked = sb.tile([P, N], U32, name="word_picked", tag="stage1", align_bytes=64)
+        word_picked = staged([P, N], U32, "word_picked", 1)
         nc.vector.tensor_copy(word_picked[:], word_table[:].bitcast(U32).indirect(offsets[:]))
         k_codes = sb.tile([P, PASSES * PACK * P * 2], U8, name="k_codes", align_bytes=64)
         nc.vector.tensor_copy(
@@ -103,7 +113,7 @@ def tile_attend_mlp_gelu_srt_kernel(tc, qT, k_words, k_scales, vT, us, offs, out
 
         v_table = []
         for j in range(V_TILES):
-            v_table.append(sb.tile([P, T], F32, name="v_table%d" % j, tag="stage%d" % j, align_bytes=64))
+            v_table.append(staged([P, T], F32, "v_table%d" % j, j))
             nc.sync.dma_start(out=v_table[j][:], in_=vT[P * j : P * (j + 1), :])
 
         y, acts = {}, {}
@@ -111,7 +121,7 @@ def tile_attend_mlp_gelu_srt_kernel(tc, qT, k_words, k_scales, vT, us, offs, out
         def first_layer(c):
             cols = slice(P * (c % 2), P * (c % 2 + 1))
             moving = [(q_mx[c // 2, o][0][:, cols], q_mx[c // 2, o][1][:, cols]) for o in range(PASSES)]
-            acc = ps.tile([P, PACK, P], F32, name="acc", tag="acc", bufs=3)
+            acc = ps.tile([P, PACK, P], F32, name="acc", tag="layer", bufs=LAYER_BANKS)
             for t in range(PACK):
                 for o in range(PASSES):
                     at = (t * PASSES + o) * 2 * P
@@ -131,15 +141,15 @@ def tile_attend_mlp_gelu_srt_kernel(tc, qT, k_words, k_scales, vT, us, offs, out
             )
 
         def gather_values(j):
-            picked = sb.tile([P, N], BF16, name="v_picked%d" % j)
-            nc.vector.tensor_copy(picked[:], v_table[j][:].indirect(offsets[:]))
-            return picked
+            columns = sb.tile([P, N], BF16, name="v_picked%d" % j)
+            nc.vector.tensor_copy(columns[:], v_table[j][:].indirect(offsets[:]))
+            return columns
 
-        def turn_values(picked, grouped):
-            words = picked[:].bitcast(F32)
-            turned = ps.tile([P, 2, P], F32, name="turned", tag="turned", bufs=2)
+        def turn_values(columns, grouped):
+            pairs = columns[:].bitcast(F32)
+            turned = ps.tile([P, 2, P], F32, name="turned", tag="layer", bufs=LAYER_BANKS)
             for u in range(2):
-                nc.tensor.transpose(turned[:, u, :], words[:, u : 2 * P : 2], ident[:])
+                nc.tensor.transpose(turned[:, u, :], pairs[:, u : 2 * P : 2], ident[:])
             nc.scalar.copy(
                 out=grouped.rearrange("p e t -> p (e t)").bitcast(F32).rearrange("p (e u) -> p e u", u=2),
                 in_=turned[:].rearrange("p u e -> p e u"),
@@ -147,17 +157,17 @@ def tile_attend_mlp_gelu_srt_kernel(tc, qT, k_words, k_scales, vT, us, offs, out
 
         out_view = out[0].rearrange("(c p) e -> p c e", p=P)
 
-        def second_layer(e0, v, chunks, copy):
-            width = v[0].shape[1]
-            acc = ps.tile([P, len(chunks), width], F32, name="res", tag="res", bufs=3)
-            for i, c in enumerate(chunks):
+        def second_layer(e0, v_mx, chunks, copy):
+            width = v_mx[0].shape[1]
+            acc = ps.tile([P, len(chunks), width], F32, name="res_acc", tag="result", bufs=RESULT_BANKS)
+            for place, c in enumerate(chunks):
                 cols = slice(P * (c % 2), P * (c % 2 + 1))
                 nc.tensor.matmul_mx(
-                    out=acc[:, i, :],
+                    out=acc[:, place, :],
                     lhsT=y_mx[c // 2][0][:, cols].bitcast(FP8X4),
                     lhsT_scale=y_mx[c // 2][1][:, cols],
-                    rhs=v[0][:].bitcast(FP8X4),
-                    rhs_scale=v[1][:],
+                    rhs=v_mx[0][:].bitcast(FP8X4),
+                    rhs_scale=v_mx[1][:],
                     start=True,
                     stop=True,
                 )
@@ -165,25 +175,31 @@ def tile_attend_mlp_gelu_srt_kernel(tc, qT, k_words, k_scales, vT, us, offs, out
             copy(out=res[:], in_=acc[:])
             nc.sync.dma_start(out=out_view[:, chunks[0] : chunks[-1] + 1, e0 : e0 + width], in_=res[:])
 
-        y_mx = []
+        picked = [gather_values(0)]
+        y[0] = staged([P, HALF, PACK], BF16, "y0", 0)
+        acts[0] = staged([P, HALF, PACK], F32, "act0", 4)
+        first_layer(0)
+        first_layer(1)
+        picked.append(gather_values(1))
+        y_mx = [quantize(nc, sb, y[0][:], "y0", staged([P, HALF], U32, "y0_codes", 1, BUFFER // 2))]
+        y[1] = staged([P, HALF, PACK], BF16, "y1", 1)
+        acts[1] = sb.tile([P, HALF, PACK], F32, name="act1")
+        first_layer(2)
+        first_layer(3)
         v01 = sb.tile([P, 2 * P, PACK], BF16, name="v01", align_bytes=64)
-        for h in range(2):
-            picked = gather_values(h)
-            y[h] = sb.tile([P, HALF, PACK], BF16, name="y%d" % h, tag="stage%d" % h, align_bytes=64)
-            acts[h] = sb.tile([P, HALF, PACK], F32, name="act%d" % h, tag=["stage4", "act1"][h], align_bytes=64)
-            first_layer(2 * h)
-            first_layer(2 * h + 1)
-            y_mx.append(quantize(nc, sb, y[h][:], "y%d" % h))
-            turn_values(picked, v01[:, P * h : P * (h + 1), :])
-        v01_mx = quantize(nc, sb, v01[:], "v01", "stage1")
-        picked = [gather_values(j) for j in (2, 3)]
-        second_layer(0, v01_mx, [0, 1], nc.scalar.copy)
-        second_layer(0, v01_mx, [2, 3], nc.scalar.copy)
+        for j in range(2):
+            turn_values(picked[j], v01[:, P * j : P * (j + 1), :])
+        picked.append(gather_values(2))
+        y_mx.append(quantize(nc, sb, y[1][:], "y1", staged([P, HALF], U32, "y1_codes", 2)))
+        v01_mx = quantize(nc, sb, v01[:], "v01", staged([P, 2 * P], U32, "v01_codes", 2, BUFFER // 2))
+        picked.append(gather_values(3))
         v2 = sb.tile([P, P, PACK], BF16, name="v2", align_bytes=64)
         v3 = sb.tile([P, P, PACK], BF16, name="v3", align_bytes=64)
-        turn_values(picked[0], v2[:])
-        turn_values(picked[1], v3[:])
-        v2_mx = quantize(nc, sb, v2[:], "v2", "stage3")
+        turn_values(picked[2], v2[:])
+        second_layer(0, v01_mx, [0, 1], nc.scalar.copy)
+        second_layer(0, v01_mx, [2, 3], nc.scalar.copy)
+        turn_values(picked[3], v3[:])
+        v2_mx = quantize(nc, sb, v2[:], "v2", staged([P, P], U32, "v2_codes", 3))
         v3_mx = quantize(nc, sb, v3[:], "v3")
         second_layer(2 * P, v2_mx, [0, 1, 2, 3], nc.scalar.copy)
         second_layer(3 * P, v3_mx, [0, 1], nc.vector.tensor_copy)

@@ -25,9 +25,9 @@ QUADS = 4
 V_TILES = DV // P
 HALF = NQ // 2
 BUFFER = 4 * T
-MOVES_ON_SCALAR = 5
-LAYER_BANKS = 3
-RESULT_BANKS = 5
+COPY = mybir.ActivationFunctionType.Copy
+CHUNKS = NQ // P
+SPLIT = 288
 
 
 def interleave(copy, grouped, planes):
@@ -50,34 +50,33 @@ def tile_attend_mlp_gelu_srt_kernel(tc, qT, k_words, k_scales, vT, us, offs, out
         staging = ctx.enter_context(tc.tile_pool(name="staging", bufs=1))
         ps = ctx.enter_context(tc.psum_pool(name="ps", bufs=1))
 
-        def staged(shape, dtype, name, buffer, at=0):
-            return staging.tile(shape, dtype, name=name, offset=buffer * BUFFER + at, align_bytes=64)
+        def staged(shape, dtype, name, at):
+            return staging.tile(shape, dtype, name=name, offset=at, align_bytes=64)
+
+        def bank(shape, name, number):
+            return ps.tile(shape, F32, name=name, offset=number * 2048)
 
         offsets = sb.tile([P, N // 16], U16, name="offsets")
         nc.sync.dma_start(offsets[:], offs)
 
         scale_table = sb.tile([P, T], U8, name="scale_table")
-        nc.sync.dma_start(out=scale_table[0:32, :].bitcast(I32), in_=k_scales.rearrange("o f t -> (o f) t").bitcast(I32))
+        nc.sync.dma_start(out=scale_table[0:32, :].bitcast(I32), in_=k_scales.rearrange("o f t -> f o t").bitcast(I32))
         nc.vector.memset(scale_table[32:64, :].bitcast(I32), 0)
         nc.vector.memset(scale_table[64:128, :].bitcast(I32), 0)
-        k_plane = [sb.tile([P, PACK * P], U8, name="k_plane%d" % o, align_bytes=64) for o in range(PASSES)]
-        nc.vector.memset(k_plane[1][:].bitcast(I32), 0)
+        k_plane = sb.tile([P, PASSES * N], U8, name="k_plane", align_bytes=64)
+        nc.vector.memset(k_plane[:].bitcast(I32), 0)
 
         us_cols = sb.tile([P, PACK], F32, name="us_cols")
         nc.gpsimd.dma_start(out=us_cols[:], in_=us[0].rearrange("(p t) x -> p (t x)", t=PACK))
         ident = sb.tile([P, P], F32, name="ident")
         make_identity(nc, ident[:])
 
-        word_table = staged([P, T], I32, "word_table", 0)
+        word_table = staged([P, T], I32, "word_table", BUFFER // 2)
         nc.sync.dma_start(out=word_table[:], in_=k_words[0].rearrange("g t b -> g (t b)").bitcast(I32))
         q_rows = [qT[0, K_PASS * o : K_PASS * (o + 1), :].rearrange("(p t) w -> p t w", t=PACK) for o in range(PASSES)]
-        q0_raw = staged([P, PACK, NQ], F32, "q0_raw", 2)
-        nc.sync.dma_start(out=q0_raw[:], in_=q_rows[0])
-        q_raw = {(h, 0): q0_raw[:, :, HALF * h : HALF * (h + 1)] for h in range(2)}
-        for h in range(2):
-            q1_raw = staged([P, PACK, HALF], F32, "q1_raw%d" % h, 3 + h)
-            nc.sync.dma_start(out=q1_raw[:], in_=q_rows[1][:, :, HALF * h : HALF * (h + 1)])
-            q_raw[h, 1] = q1_raw[:]
+        q_raw = [sb.tile([P, PACK, NQ], F32, name="q_raw%d" % o) for o in range(PASSES)]
+        for o in range(PASSES):
+            nc.sync.dma_start(out=q_raw[o][:], in_=q_rows[o])
 
         warm = sb.tile([P, 2], F32, name="warm")
         nc.vector.memset(warm[:, 0:1], 0.0)
@@ -85,18 +84,16 @@ def tile_attend_mlp_gelu_srt_kernel(tc, qT, k_words, k_scales, vT, us, offs, out
 
         scale_picked = sb.tile([P, N], U8, name="scale_picked")
         nc.vector.tensor_copy(scale_picked[:], scale_table[:].indirect(offsets[:]))
+        scale_dealt = sb.tile([P, N], U8, name="scale_dealt")
         nc.vector.tensor_copy(
-            out=k_plane[0][:].rearrange("p (t m) -> p t m", t=PACK), in_=scale_picked[:].rearrange("p (m t) -> p t m", t=PACK)
+            out=scale_dealt[:].rearrange("p (t m) -> p t m", t=PACK), in_=scale_picked[:].rearrange("p (m t) -> p t m", t=PACK)
         )
-        moves = [(o, quad) for o in range(PASSES) for quad in range(QUADS) if (o, quad) != (0, 0)]
-        for number, (o, quad) in enumerate(moves):
-            queue = nc.scalar if number < MOVES_ON_SCALAR else nc.gpsimd
-            row = 16 * o + 4 * quad
-            queue.dma_start(
-                out=k_plane[o][32 * quad : 32 * quad + 4, :].bitcast(I32), in_=k_plane[0][row : row + 4, :].bitcast(I32)
+        for quad in range(QUADS):
+            nc.scalar.dma_start(
+                out=k_plane[32 * quad : 32 * quad + 4, :].bitcast(I32), in_=scale_dealt[8 * quad : 8 * quad + 8, :].bitcast(I32)
             )
 
-        word_picked = staged([P, N], U32, "word_picked", 1)
+        word_picked = staged([P, N], U32, "word_picked", 3 * BUFFER - 1024)
         nc.vector.tensor_copy(word_picked[:], word_table[:].bitcast(U32).indirect(offsets[:]))
         k_codes = sb.tile([P, PASSES * PACK * P * 2], U8, name="k_codes", align_bytes=64)
         nc.vector.tensor_copy(
@@ -104,66 +101,77 @@ def tile_attend_mlp_gelu_srt_kernel(tc, qT, k_words, k_scales, vT, us, offs, out
             in_=word_picked[:].bitcast(U16).rearrange("p (m t o) -> p t m o", t=PACK, o=PASSES),
         )
 
-        q_mx = {}
-        for h, copy in enumerate([nc.vector.tensor_copy, nc.scalar.copy]):
-            for o in range(PASSES):
-                grouped = sb.tile([P, HALF, PACK], BF16, name="q_grouped%d_%d" % (h, o), align_bytes=64)
-                interleave(copy, grouped[:], q_raw[h, o])
-                q_mx[h, o] = quantize(nc, sb, grouped[:], "q%d_%d" % (h, o))
-
         v_table = []
         for j in range(V_TILES):
-            v_table.append(staged([P, T], F32, "v_table%d" % j, j))
+            v_table.append(staged([P, T], F32, "v_table%d" % j, j * BUFFER))
             nc.sync.dma_start(out=v_table[j][:], in_=vT[P * j : P * (j + 1), :])
 
-        y, acts = {}, {}
-
-        def first_layer(c):
-            cols = slice(P * (c % 2), P * (c % 2 + 1))
-            moving = [(q_mx[c // 2, o][0][:, cols], q_mx[c // 2, o][1][:, cols]) for o in range(PASSES)]
-            acc = ps.tile([P, PACK, P], F32, name="acc", tag="layer", bufs=LAYER_BANKS)
-            for t in range(PACK):
-                for o in range(PASSES):
+        work = 4 * BUFFER
+        acc = [bank([P, PACK, P], "acc%d" % c, c) for c in range(CHUNKS)]
+        q_mx = {}
+        for o in range(PASSES):
+            grouped = [staged([P, HALF, PACK], BF16, "q_grouped%d_%d" % (h, o), work + 2048 * (2 * o + h)) for h in range(2)]
+            interleave(nc.vector.tensor_copy, grouped[0][:], q_raw[o][:, :, 0:HALF])
+            interleave(nc.vector.tensor_copy, grouped[1][:, 0:P, :], q_raw[o][:, :, HALF : HALF + P])
+            interleave(nc.scalar.copy, grouped[1][:, P:HALF, :], q_raw[o][:, :, HALF + P : NQ])
+            for h in range(2):
+                q_mx[h, o] = quantize(nc, sb, grouped[h][:], "q%d_%d" % (h, o))
+            for c in range(CHUNKS):
+                cols = slice(P * (c % 2), P * (c % 2 + 1))
+                for t in range(PACK):
                     at = (t * PASSES + o) * 2 * P
                     nc.tensor.matmul_mx(
-                        out=acc[:, t, :],
+                        out=acc[c][:, t, :],
                         lhsT=k_codes[:, at : at + 2 * P].bitcast(FP4X4),
-                        lhsT_scale=k_plane[o][:, P * t : P * (t + 1)],
-                        rhs=moving[o][0].bitcast(FP8X4),
-                        rhs_scale=moving[o][1],
-                        start=(o == 0),
-                        stop=(o == PASSES - 1),
+                        lhsT_scale=k_plane[:, N * o + P * t : N * o + P * (t + 1)],
+                        rhs=q_mx[c // 2, o][0][:, cols].bitcast(FP8X4),
+                        rhs_scale=q_mx[c // 2, o][1][:, cols],
+                        start=(o == 0 and t == 0),
+                        stop=(o == PASSES - 1 and t == PACK - 1),
                     )
-            act = acts[c // 2][:, cols, :]
-            nc.scalar.activation(out=act, in_=acc[:].rearrange("p t q -> p q t"), func=GELU)
+
+        late = 5 * BUFFER
+        y = [staged([P, HALF, PACK], BF16, "y%d" % h, late + 2048 * h) for h in range(2)]
+        acts = [staged([P, P, PACK], F32, "act%d" % c, 7 * BUFFER + 2048 * c) for c in range(CHUNKS)]
+        for c in range(CHUNKS):
+            nc.scalar.activation(out=acts[c][:], in_=acc[c][:].rearrange("p t q -> p q t"), func=GELU)
+
+        def scale_rows(c):
             nc.vector.tensor_tensor(
-                out=y[c // 2][:, cols, :], in0=act, in1=us_cols[:].unsqueeze(1).to_broadcast([P, P, PACK]), op=MULT
+                out=y[c // 2][:, P * (c % 2) : P * (c % 2 + 1), :],
+                in0=acts[c][:],
+                in1=us_cols[:].unsqueeze(1).to_broadcast([P, P, PACK]),
+                op=MULT,
             )
 
-        def gather_values(j):
-            columns = sb.tile([P, N], BF16, name="v_picked%d" % j)
-            nc.vector.tensor_copy(columns[:], v_table[j][:].indirect(offsets[:]))
-            return columns
+        picked_at = [work + 2048 * 3, 7 * BUFFER + 2048, late + 2048, 9 * BUFFER + 1024]
+        picked = [staged([P, N], BF16, "v_picked%d" % j, picked_at[j]) for j in range(V_TILES)]
 
-        def turn_values(columns, grouped):
-            pairs = columns[:].bitcast(F32)
-            turned = ps.tile([P, 2, P], F32, name="turned", tag="layer", bufs=LAYER_BANKS)
+        def gather_on_vector(j, a, b):
+            nc.vector.tensor_copy(picked[j][:, a:b], v_table[j][:].indirect(offsets[:, a // 16 : b // 16]))
+
+        def gather_on_scalar(j, a, b):
+            nc.scalar.activation(picked[j][:, a:b], v_table[j][:].indirect(offsets[:, a // 16 : b // 16]), COPY)
+
+        def turn_values(j, grouped, number, copy):
+            pairs = picked[j][:].bitcast(F32)
+            turned = bank([P, 2, P], "turned%d" % j, number)
             for u in range(2):
                 nc.tensor.transpose(turned[:, u, :], pairs[:, u : 2 * P : 2], ident[:])
-            nc.scalar.copy(
+            copy(
                 out=grouped.rearrange("p e t -> p (e t)").bitcast(F32).rearrange("p (e u) -> p e u", u=2),
                 in_=turned[:].rearrange("p u e -> p e u"),
             )
 
         out_view = out[0].rearrange("(c p) e -> p c e", p=P)
 
-        def second_layer(e0, v_mx, chunks, copy):
+        def second_layer(e0, v_mx, chunks, copy, number, at):
             width = v_mx[0].shape[1]
-            acc = ps.tile([P, len(chunks), width], F32, name="res_acc", tag="result", bufs=RESULT_BANKS)
+            res_acc = bank([P, len(chunks), width], "res_acc%d_%d" % (e0, chunks[0]), number)
             for place, c in enumerate(chunks):
                 cols = slice(P * (c % 2), P * (c % 2 + 1))
                 nc.tensor.matmul_mx(
-                    out=acc[:, place, :],
+                    out=res_acc[:, place, :],
                     lhsT=y_mx[c // 2][0][:, cols].bitcast(FP8X4),
                     lhsT_scale=y_mx[c // 2][1][:, cols],
                     rhs=v_mx[0][:].bitcast(FP8X4),
@@ -171,36 +179,33 @@ def tile_attend_mlp_gelu_srt_kernel(tc, qT, k_words, k_scales, vT, us, offs, out
                     start=True,
                     stop=True,
                 )
-            res = sb.tile([P, len(chunks), width], F32, name="res%d_%d" % (e0, chunks[0]))
-            copy(out=res[:], in_=acc[:])
+            res = staged([P, len(chunks), width], F32, "res%d_%d" % (e0, chunks[0]), at)
+            copy(out=res[:], in_=res_acc[:])
             nc.sync.dma_start(out=out_view[:, chunks[0] : chunks[-1] + 1, e0 : e0 + width], in_=res[:])
 
-        picked = [gather_values(0)]
-        y[0] = staged([P, HALF, PACK], BF16, "y0", 0)
-        acts[0] = staged([P, HALF, PACK], F32, "act0", 4)
-        first_layer(0)
-        first_layer(1)
-        picked.append(gather_values(1))
-        y_mx = [quantize(nc, sb, y[0][:], "y0", staged([P, HALF], U32, "y0_codes", 1, BUFFER // 2))]
-        y[1] = staged([P, HALF, PACK], BF16, "y1", 1)
-        acts[1] = sb.tile([P, HALF, PACK], F32, name="act1")
-        first_layer(2)
-        first_layer(3)
-        v01 = sb.tile([P, 2 * P, PACK], BF16, name="v01", align_bytes=64)
-        for j in range(2):
-            turn_values(picked[j], v01[:, P * j : P * (j + 1), :])
-        picked.append(gather_values(2))
-        y_mx.append(quantize(nc, sb, y[1][:], "y1", staged([P, HALF], U32, "y1_codes", 2)))
-        v01_mx = quantize(nc, sb, v01[:], "v01", staged([P, 2 * P], U32, "v01_codes", 2, BUFFER // 2))
-        picked.append(gather_values(3))
-        v2 = sb.tile([P, P, PACK], BF16, name="v2", align_bytes=64)
-        v3 = sb.tile([P, P, PACK], BF16, name="v3", align_bytes=64)
-        turn_values(picked[2], v2[:])
-        second_layer(0, v01_mx, [0, 1], nc.scalar.copy)
-        second_layer(0, v01_mx, [2, 3], nc.scalar.copy)
-        turn_values(picked[3], v3[:])
-        v2_mx = quantize(nc, sb, v2[:], "v2", staged([P, P], U32, "v2_codes", 3))
-        v3_mx = quantize(nc, sb, v3[:], "v3")
-        second_layer(2 * P, v2_mx, [0, 1, 2, 3], nc.scalar.copy)
-        second_layer(3 * P, v3_mx, [0, 1], nc.vector.tensor_copy)
-        second_layer(3 * P, v3_mx, [2, 3], nc.scalar.copy)
+        every = list(range(CHUNKS))
+        results = 8 * BUFFER
+        v_at = [9 * BUFFER, 9 * BUFFER + 1024, 3 * BUFFER + 4096, 9 * BUFFER + 2048]
+        v = [staged([P, P, PACK], BF16, "v%d" % j, v_at[j]) for j in range(V_TILES)]
+        gather_on_vector(0, 0, N)
+        for c in every:
+            scale_rows(c)
+        turn_values(0, v[0][:], 4, nc.scalar.copy)
+        gather_on_scalar(1, 0, N)
+        y_mx = [quantize(nc, sb, y[0][:], "y0")]
+        v0_mx = quantize(nc, sb, v[0][:], "v0")
+        y_mx.append(quantize(nc, sb, y[1][:], "y1"))
+        gather_on_vector(2, 0, N)
+        turn_values(1, v[1][:], 5, nc.scalar.copy)
+        second_layer(0, v0_mx, every, nc.scalar.copy, 0, results)
+        v1_mx = quantize(nc, sb, v[1][:], "v1", staged([P, P], U32, "v1_codes", 2 * BUFFER))
+        gather_on_vector(3, 0, SPLIT)
+        gather_on_scalar(3, SPLIT, N)
+        turn_values(2, v[2][:], 6, nc.scalar.copy)
+        second_layer(P, v1_mx, every, nc.vector.tensor_copy, 1, 3 * BUFFER)
+        turn_values(3, v[3][:], 7, nc.scalar.copy)
+        v2_mx = quantize(nc, sb, v[2][:], "v2")
+        v3_mx = quantize(nc, sb, v[3][:], "v3")
+        second_layer(2 * P, v2_mx, every, nc.scalar.copy, 2, results + 2048)
+        second_layer(3 * P, v3_mx, [0, 1], nc.vector.tensor_copy, 3, results + 4096)
+        second_layer(3 * P, v3_mx, [2, 3], nc.scalar.copy, 4, results + 5120)

@@ -25,9 +25,7 @@ QUADS = 4
 V_TILES = DV // P
 HALF = NQ // 2
 BUFFER = 4 * T
-COPY = mybir.ActivationFunctionType.Copy
 CHUNKS = NQ // P
-SPLIT = 288
 
 
 def interleave(copy, grouped, planes):
@@ -112,8 +110,7 @@ def tile_attend_mlp_gelu_srt_kernel(tc, qT, k_words, k_scales, vT, us, offs, out
         for o in range(PASSES):
             grouped = [staged([P, HALF, PACK], BF16, "q_grouped%d_%d" % (h, o), work + 2048 * (2 * o + h)) for h in range(2)]
             interleave(nc.vector.tensor_copy, grouped[0][:], q_raw[o][:, :, 0:HALF])
-            interleave(nc.vector.tensor_copy, grouped[1][:, 0:P, :], q_raw[o][:, :, HALF : HALF + P])
-            interleave(nc.scalar.copy, grouped[1][:, P:HALF, :], q_raw[o][:, :, HALF + P : NQ])
+            interleave(nc.scalar.copy, grouped[1][:], q_raw[o][:, :, HALF:NQ])
             for h in range(2):
                 q_mx[h, o] = quantize(nc, sb, grouped[h][:], "q%d_%d" % (h, o))
             for c in range(CHUNKS):
@@ -144,14 +141,11 @@ def tile_attend_mlp_gelu_srt_kernel(tc, qT, k_words, k_scales, vT, us, offs, out
                 op=MULT,
             )
 
-        picked_at = [work + 2048 * 3, 7 * BUFFER + 2048, late + 2048, 9 * BUFFER + 1024]
+        picked_at = [work + 2048 * 3, late + 2048, BUFFER, 9 * BUFFER + 1024]
         picked = [staged([P, N], BF16, "v_picked%d" % j, picked_at[j]) for j in range(V_TILES)]
 
         def gather_on_vector(j, a, b):
             nc.vector.tensor_copy(picked[j][:, a:b], v_table[j][:].indirect(offsets[:, a // 16 : b // 16]))
-
-        def gather_on_scalar(j, a, b):
-            nc.scalar.activation(picked[j][:, a:b], v_table[j][:].indirect(offsets[:, a // 16 : b // 16]), COPY)
 
         def turn_values(j, grouped, number, copy):
             pairs = picked[j][:].bitcast(F32)
@@ -185,27 +179,26 @@ def tile_attend_mlp_gelu_srt_kernel(tc, qT, k_words, k_scales, vT, us, offs, out
 
         every = list(range(CHUNKS))
         results = 8 * BUFFER
-        v_at = [9 * BUFFER, 9 * BUFFER + 1024, 3 * BUFFER + 4096, 9 * BUFFER + 2048]
+        v_at = [9 * BUFFER + 1024 * j for j in range(V_TILES)]
         v = [staged([P, P, PACK], BF16, "v%d" % j, v_at[j]) for j in range(V_TILES)]
         gather_on_vector(0, 0, N)
         for c in every:
             scale_rows(c)
         turn_values(0, v[0][:], 4, nc.scalar.copy)
-        gather_on_scalar(1, 0, N)
         y_mx = [quantize(nc, sb, y[0][:], "y0")]
         v0_mx = quantize(nc, sb, v[0][:], "v0")
         y_mx.append(quantize(nc, sb, y[1][:], "y1"))
+        gather_on_vector(1, 0, N)
         gather_on_vector(2, 0, N)
-        turn_values(1, v[1][:], 5, nc.scalar.copy)
         second_layer(0, v0_mx, every, nc.scalar.copy, 0, results)
+        turn_values(1, v[1][:], 5, nc.scalar.copy)
         v1_mx = quantize(nc, sb, v[1][:], "v1", staged([P, P], U32, "v1_codes", 2 * BUFFER))
-        gather_on_vector(3, 0, SPLIT)
-        gather_on_scalar(3, SPLIT, N)
+        gather_on_vector(3, 0, N)
         turn_values(2, v[2][:], 6, nc.scalar.copy)
-        second_layer(P, v1_mx, every, nc.vector.tensor_copy, 1, 3 * BUFFER)
+        second_layer(P, v1_mx, every, nc.scalar.copy, 1, results + 6144)
+        v2_mx = quantize(nc, sb, v[2][:], "v2", staged([P, P], U32, "v2_codes", 3 * BUFFER))
         turn_values(3, v[3][:], 7, nc.scalar.copy)
-        v2_mx = quantize(nc, sb, v[2][:], "v2")
+        second_layer(2 * P, v2_mx, every, nc.vector.tensor_copy, 2, results + 2048)
         v3_mx = quantize(nc, sb, v[3][:], "v3")
-        second_layer(2 * P, v2_mx, every, nc.scalar.copy, 2, results + 2048)
         second_layer(3 * P, v3_mx, [0, 1], nc.vector.tensor_copy, 3, results + 4096)
         second_layer(3 * P, v3_mx, [2, 3], nc.scalar.copy, 4, results + 5120)

@@ -57,12 +57,12 @@ def tile_attend_mlp_gelu_srt_kernel(tc, qT, k_words, k_scales, vT, us, offs, out
         offsets = sb.tile([P, N // 16], U16, name="offsets")
         nc.sync.dma_start(offsets[:], offs)
 
-        scale_table = sb.tile([P, T], U8, name="scale_table")
+        scale_table = staged([P, T], U8, "scale_table", 6 * BUFFER)
         nc.sync.dma_start(out=scale_table[0:32, :].bitcast(I32), in_=k_scales.rearrange("o f t -> f o t").bitcast(I32))
         nc.vector.memset(scale_table[32:64, :].bitcast(I32), 0)
         nc.vector.memset(scale_table[64:128, :].bitcast(I32), 0)
-        k_plane = sb.tile([P, PASSES * N], U8, name="k_plane", align_bytes=64)
-        nc.vector.memset(k_plane[:].bitcast(I32), 0)
+        scale_placed = staged([P, PASSES * N], U8, "scale_placed", 10 * BUFFER)
+        nc.vector.memset(scale_placed[:].bitcast(I32), 0)
 
         us_cols = sb.tile([P, PACK], F32, name="us_cols")
         nc.gpsimd.dma_start(out=us_cols[:], in_=us[0].rearrange("(p t) x -> p (t x)", t=PACK))
@@ -72,9 +72,8 @@ def tile_attend_mlp_gelu_srt_kernel(tc, qT, k_words, k_scales, vT, us, offs, out
         word_table = staged([P, T], I32, "word_table", BUFFER // 2)
         nc.sync.dma_start(out=word_table[:], in_=k_words[0].rearrange("g t b -> g (t b)").bitcast(I32))
         q_rows = [qT[0, K_PASS * o : K_PASS * (o + 1), :].rearrange("(p t) w -> p t w", t=PACK) for o in range(PASSES)]
-        q_raw = [sb.tile([P, PACK, NQ], F32, name="q_raw%d" % o) for o in range(PASSES)]
-        for o in range(PASSES):
-            nc.sync.dma_start(out=q_raw[o][:], in_=q_rows[o])
+        q_raw = [sb.tile([P, PACK, NQ], F32, name="q_raw0")]
+        nc.sync.dma_start(out=q_raw[0][:], in_=q_rows[0])
 
         warm = sb.tile([P, 2], F32, name="warm")
         nc.vector.memset(warm[:, 0:1], 0.0)
@@ -82,14 +81,13 @@ def tile_attend_mlp_gelu_srt_kernel(tc, qT, k_words, k_scales, vT, us, offs, out
 
         scale_picked = sb.tile([P, N], U8, name="scale_picked")
         nc.vector.tensor_copy(scale_picked[:], scale_table[:].indirect(offsets[:]))
-        scale_dealt = sb.tile([P, N], U8, name="scale_dealt")
-        nc.vector.tensor_copy(
-            out=scale_dealt[:].rearrange("p (t m) -> p t m", t=PACK), in_=scale_picked[:].rearrange("p (m t) -> p t m", t=PACK)
-        )
         for quad in range(QUADS):
-            nc.scalar.dma_start(
-                out=k_plane[32 * quad : 32 * quad + 4, :].bitcast(I32), in_=scale_dealt[8 * quad : 8 * quad + 8, :].bitcast(I32)
+            nc.sync.dma_start(
+                out=scale_placed[32 * quad : 32 * quad + 4, :].bitcast(I32),
+                in_=scale_picked[8 * quad : 8 * quad + 8, :].bitcast(I32),
             )
+        q_raw.append(staged([P, PACK, NQ], F32, "q_raw1", 6 * BUFFER))
+        nc.sync.dma_start(out=q_raw[1][:], in_=q_rows[1])
 
         word_picked = staged([P, N], U32, "word_picked", 3 * BUFFER - 1024)
         nc.vector.tensor_copy(word_picked[:], word_table[:].bitcast(U32).indirect(offsets[:]))
@@ -107,12 +105,19 @@ def tile_attend_mlp_gelu_srt_kernel(tc, qT, k_words, k_scales, vT, us, offs, out
         work = 4 * BUFFER
         acc = [bank([P, PACK, P], "acc%d" % c, c) for c in range(CHUNKS)]
         q_mx = {}
+        k_plane = sb.tile([P, PASSES * N], U8, name="k_plane", align_bytes=64)
         for o in range(PASSES):
             grouped = [staged([P, HALF, PACK], BF16, "q_grouped%d_%d" % (h, o), work + 2048 * (2 * o + h)) for h in range(2)]
             interleave(nc.vector.tensor_copy, grouped[0][:], q_raw[o][:, :, 0:HALF])
             interleave(nc.scalar.copy, grouped[1][:], q_raw[o][:, :, HALF:NQ])
+            if o == 0:
+                nc.vector.tensor_copy(
+                    out=k_plane[:].rearrange("p (o t m) -> p o t m", o=PASSES, t=PACK),
+                    in_=scale_placed[:].rearrange("p (o m t) -> p o t m", o=PASSES, t=PACK),
+                )
             for h in range(2):
-                q_mx[h, o] = quantize(nc, sb, grouped[h][:], "q%d_%d" % (h, o))
+                codes = staged([P, HALF], U32, "q_codes%d_%d" % (h, o), 10 * BUFFER + 1024 * (2 * o + 1 - h))
+                q_mx[h, o] = quantize(nc, sb, grouped[h][:], "q%d_%d" % (h, o), codes)
             for c in range(CHUNKS):
                 cols = slice(P * (c % 2), P * (c % 2 + 1))
                 for t in range(PACK):
@@ -128,16 +133,18 @@ def tile_attend_mlp_gelu_srt_kernel(tc, qT, k_words, k_scales, vT, us, offs, out
                     )
 
         late = 5 * BUFFER
-        y = [staged([P, HALF, PACK], BF16, "y%d" % h, late + 2048 * h) for h in range(2)]
-        acts = [staged([P, P, PACK], F32, "act%d" % c, 7 * BUFFER + 2048 * c) for c in range(CHUNKS)]
+        y = staged([P, NQ, PACK], BF16, "y", late)
+        acts = [staged([P, HALF, PACK], F32, "act%d" % h, 7 * BUFFER + 4096 * h) for h in range(2)]
         for c in range(CHUNKS):
-            nc.scalar.activation(out=acts[c][:], in_=acc[c][:].rearrange("p t q -> p q t"), func=GELU)
+            nc.scalar.activation(
+                out=acts[c // 2][:, P * (c % 2) : P * (c % 2 + 1), :], in_=acc[c][:].rearrange("p t q -> p q t"), func=GELU
+            )
 
-        def scale_rows(c):
+        def scale_rows(h):
             nc.vector.tensor_tensor(
-                out=y[c // 2][:, P * (c % 2) : P * (c % 2 + 1), :],
-                in0=acts[c][:],
-                in1=us_cols[:].unsqueeze(1).to_broadcast([P, P, PACK]),
+                out=y[:, HALF * h : HALF * (h + 1), :],
+                in0=acts[h][:],
+                in1=us_cols[:].unsqueeze(1).to_broadcast([P, HALF, PACK]),
                 op=MULT,
             )
 
@@ -163,11 +170,11 @@ def tile_attend_mlp_gelu_srt_kernel(tc, qT, k_words, k_scales, vT, us, offs, out
             width = v_mx[0].shape[1]
             res_acc = bank([P, len(chunks), width], "res_acc%d_%d" % (e0, chunks[0]), number)
             for place, c in enumerate(chunks):
-                cols = slice(P * (c % 2), P * (c % 2 + 1))
+                cols = slice(P * c, P * (c + 1))
                 nc.tensor.matmul_mx(
                     out=res_acc[:, place, :],
-                    lhsT=y_mx[c // 2][0][:, cols].bitcast(FP8X4),
-                    lhsT_scale=y_mx[c // 2][1][:, cols],
+                    lhsT=y_mx[0][:, cols].bitcast(FP8X4),
+                    lhsT_scale=y_mx[1][:, cols],
                     rhs=v_mx[0][:].bitcast(FP8X4),
                     rhs_scale=v_mx[1][:],
                     start=True,
@@ -182,12 +189,11 @@ def tile_attend_mlp_gelu_srt_kernel(tc, qT, k_words, k_scales, vT, us, offs, out
         v_at = [9 * BUFFER + 1024 * j for j in range(V_TILES)]
         v = [staged([P, P, PACK], BF16, "v%d" % j, v_at[j]) for j in range(V_TILES)]
         gather_on_vector(0, 0, N)
-        for c in every:
-            scale_rows(c)
+        for h in range(2):
+            scale_rows(h)
         turn_values(0, v[0][:], 4, nc.scalar.copy)
-        y_mx = [quantize(nc, sb, y[0][:], "y0")]
         v0_mx = quantize(nc, sb, v[0][:], "v0")
-        y_mx.append(quantize(nc, sb, y[1][:], "y1"))
+        y_mx = quantize(nc, sb, y[:], "y")
         gather_on_vector(1, 0, N)
         gather_on_vector(2, 0, N)
         second_layer(0, v0_mx, every, nc.scalar.copy, 0, results)
@@ -198,7 +204,7 @@ def tile_attend_mlp_gelu_srt_kernel(tc, qT, k_words, k_scales, vT, us, offs, out
         second_layer(P, v1_mx, every, nc.scalar.copy, 1, results + 6144)
         v2_mx = quantize(nc, sb, v[2][:], "v2", staged([P, P], U32, "v2_codes", 3 * BUFFER))
         turn_values(3, v[3][:], 7, nc.scalar.copy)
-        second_layer(2 * P, v2_mx, every, nc.vector.tensor_copy, 2, results + 2048)
         v3_mx = quantize(nc, sb, v[3][:], "v3")
+        second_layer(2 * P, v2_mx, every, nc.scalar.copy, 2, results + 2048)
         second_layer(3 * P, v3_mx, [0, 1], nc.vector.tensor_copy, 3, results + 4096)
         second_layer(3 * P, v3_mx, [2, 3], nc.scalar.copy, 4, results + 5120)

@@ -26,6 +26,7 @@ V_TILES = DV // P
 HALF = NQ // 2
 BUFFER = 4 * T
 CHUNKS = NQ // P
+MOVES_ON_SYNC = 6
 
 
 def interleave(copy, grouped, planes):
@@ -58,11 +59,12 @@ def tile_attend_mlp_gelu_srt_kernel(tc, qT, k_words, k_scales, vT, us, offs, out
         nc.sync.dma_start(offsets[:], offs)
 
         scale_table = staged([P, T], U8, "scale_table", 6 * BUFFER)
-        nc.sync.dma_start(out=scale_table[0:32, :].bitcast(I32), in_=k_scales.rearrange("o f t -> f o t").bitcast(I32))
+        nc.sync.dma_start(out=scale_table[0:32, :].bitcast(I32), in_=k_scales.rearrange("o f t -> (o f) t").bitcast(I32))
         nc.vector.memset(scale_table[32:64, :].bitcast(I32), 0)
         nc.vector.memset(scale_table[64:128, :].bitcast(I32), 0)
-        scale_placed = staged([P, PASSES * N], U8, "scale_placed", 10 * BUFFER)
-        nc.vector.memset(scale_placed[:].bitcast(I32), 0)
+        scale_placed = [staged([P, N], U8, "scale_placed%d" % o, 10 * BUFFER + 4096 * o) for o in range(PASSES)]
+        for o in range(PASSES):
+            nc.vector.memset(scale_placed[o][:].bitcast(I32), 0)
 
         us_cols = sb.tile([P, PACK], F32, name="us_cols")
         nc.gpsimd.dma_start(out=us_cols[:], in_=us[0].rearrange("(p t) x -> p (t x)", t=PACK))
@@ -81,11 +83,15 @@ def tile_attend_mlp_gelu_srt_kernel(tc, qT, k_words, k_scales, vT, us, offs, out
 
         scale_picked = sb.tile([P, N], U8, name="scale_picked")
         nc.vector.tensor_copy(scale_picked[:], scale_table[:].indirect(offsets[:]))
-        for quad in range(QUADS):
-            nc.sync.dma_start(
-                out=scale_placed[32 * quad : 32 * quad + 4, :].bitcast(I32),
-                in_=scale_picked[8 * quad : 8 * quad + 8, :].bitcast(I32),
+        moves = [(o, quad) for o in range(PASSES) for quad in range(QUADS) if (o, quad) != (0, 0)]
+        for number, (o, quad) in enumerate(moves):
+            queue = nc.sync if number < MOVES_ON_SYNC else nc.gpsimd
+            row = 16 * o + 4 * quad
+            queue.dma_start(
+                out=scale_placed[o][32 * quad : 32 * quad + 4, :].bitcast(I32),
+                in_=scale_picked[row : row + 4, :].bitcast(I32),
             )
+        nc.vector.tensor_copy(scale_placed[0][0:32, :].bitcast(I32), scale_picked[0:32, :].bitcast(I32))
         q_raw.append(staged([P, PACK, NQ], F32, "q_raw1", 6 * BUFFER))
         nc.sync.dma_start(out=q_raw[1][:], in_=q_rows[1])
 
@@ -105,18 +111,17 @@ def tile_attend_mlp_gelu_srt_kernel(tc, qT, k_words, k_scales, vT, us, offs, out
         work = 4 * BUFFER
         acc = [bank([P, PACK, P], "acc%d" % c, c) for c in range(CHUNKS)]
         q_mx = {}
-        k_plane = sb.tile([P, PASSES * N], U8, name="k_plane", align_bytes=64)
+        k_plane = [sb.tile([P, N], U8, name="k_plane%d" % o, align_bytes=64) for o in range(PASSES)]
         for o in range(PASSES):
             grouped = [staged([P, HALF, PACK], BF16, "q_grouped%d_%d" % (h, o), work + 2048 * (2 * o + h)) for h in range(2)]
             interleave(nc.vector.tensor_copy, grouped[0][:], q_raw[o][:, :, 0:HALF])
             interleave(nc.scalar.copy, grouped[1][:], q_raw[o][:, :, HALF:NQ])
-            if o == 0:
-                nc.vector.tensor_copy(
-                    out=k_plane[:].rearrange("p (o t m) -> p o t m", o=PASSES, t=PACK),
-                    in_=scale_placed[:].rearrange("p (o m t) -> p o t m", o=PASSES, t=PACK),
-                )
+            nc.vector.tensor_copy(
+                out=k_plane[o][:].rearrange("p (t m) -> p t m", t=PACK),
+                in_=scale_placed[o][:].rearrange("p (m t) -> p t m", t=PACK),
+            )
             for h in range(2):
-                codes = staged([P, HALF], U32, "q_codes%d_%d" % (h, o), 10 * BUFFER + 1024 * (2 * o + 1 - h))
+                codes = staged([P, HALF], U32, "q_codes%d_%d" % (h, o), 10 * BUFFER + 4096 * o + 1024 * ((h + o + 1) % 2))
                 q_mx[h, o] = quantize(nc, sb, grouped[h][:], "q%d_%d" % (h, o), codes)
             for c in range(CHUNKS):
                 cols = slice(P * (c % 2), P * (c % 2 + 1))
@@ -125,7 +130,7 @@ def tile_attend_mlp_gelu_srt_kernel(tc, qT, k_words, k_scales, vT, us, offs, out
                     nc.tensor.matmul_mx(
                         out=acc[c][:, t, :],
                         lhsT=k_codes[:, at : at + 2 * P].bitcast(FP4X4),
-                        lhsT_scale=k_plane[:, N * o + P * t : N * o + P * (t + 1)],
+                        lhsT_scale=k_plane[o][:, P * t : P * (t + 1)],
                         rhs=q_mx[c // 2, o][0][:, cols].bitcast(FP8X4),
                         rhs_scale=q_mx[c // 2, o][1][:, cols],
                         start=(o == 0 and t == 0),

@@ -26,6 +26,8 @@ V_TILES = DV // P
 HALF = NQ // 2
 BUFFER = 4 * T
 CHUNKS = NQ // P
+COPY = mybir.ActivationFunctionType.Copy
+SPLIT = 288
 MOVES_ON_SYNC = 6
 
 
@@ -153,11 +155,14 @@ def tile_attend_mlp_gelu_srt_kernel(tc, qT, k_words, k_scales, vT, us, offs, out
                 op=MULT,
             )
 
-        picked_at = [work + 2048 * 3, late + 2048, BUFFER, 9 * BUFFER + 1024]
+        picked_at = [work + 2048 * 3, 7 * BUFFER, 11 * BUFFER, 11 * BUFFER + 1024]
         picked = [staged([P, N], BF16, "v_picked%d" % j, picked_at[j]) for j in range(V_TILES)]
 
         def gather_on_vector(j, a, b):
             nc.vector.tensor_copy(picked[j][:, a:b], v_table[j][:].indirect(offsets[:, a // 16 : b // 16]))
+
+        def gather_on_scalar(j, a, b):
+            nc.scalar.activation(picked[j][:, a:b], v_table[j][:].indirect(offsets[:, a // 16 : b // 16]), COPY)
 
         def turn_values(j, grouped, number, copy):
             pairs = picked[j][:].bitcast(F32)
@@ -191,24 +196,25 @@ def tile_attend_mlp_gelu_srt_kernel(tc, qT, k_words, k_scales, vT, us, offs, out
 
         every = list(range(CHUNKS))
         results = 8 * BUFFER
-        v_at = [9 * BUFFER + 1024 * j for j in range(V_TILES)]
+        v_at = [9 * BUFFER, 9 * BUFFER + 1024, 3 * BUFFER + 4096, 9 * BUFFER + 2048]
         v = [staged([P, P, PACK], BF16, "v%d" % j, v_at[j]) for j in range(V_TILES)]
         gather_on_vector(0, 0, N)
         for h in range(2):
             scale_rows(h)
         turn_values(0, v[0][:], 4, nc.scalar.copy)
+        gather_on_scalar(1, 0, N)
         v0_mx = quantize(nc, sb, v[0][:], "v0")
         y_mx = quantize(nc, sb, y[:], "y")
-        gather_on_vector(1, 0, N)
         gather_on_vector(2, 0, N)
-        second_layer(0, v0_mx, every, nc.scalar.copy, 0, results)
         turn_values(1, v[1][:], 5, nc.scalar.copy)
+        second_layer(0, v0_mx, every, nc.scalar.copy, 0, results)
         v1_mx = quantize(nc, sb, v[1][:], "v1", staged([P, P], U32, "v1_codes", 2 * BUFFER))
-        gather_on_vector(3, 0, N)
+        gather_on_vector(3, 0, SPLIT)
+        gather_on_scalar(3, SPLIT, N)
         turn_values(2, v[2][:], 6, nc.scalar.copy)
-        second_layer(P, v1_mx, every, nc.scalar.copy, 1, results + 6144)
-        v2_mx = quantize(nc, sb, v[2][:], "v2", staged([P, P], U32, "v2_codes", 3 * BUFFER))
+        second_layer(P, v1_mx, every, nc.vector.tensor_copy, 1, 3 * BUFFER)
         turn_values(3, v[3][:], 7, nc.scalar.copy)
+        v2_mx = quantize(nc, sb, v[2][:], "v2")
         v3_mx = quantize(nc, sb, v[3][:], "v3")
         second_layer(2 * P, v2_mx, every, nc.scalar.copy, 2, results + 2048)
         second_layer(3 * P, v3_mx, [0, 1], nc.vector.tensor_copy, 3, results + 4096)

@@ -27,8 +27,7 @@ HALF = NQ // 2
 BUFFER = 4 * T
 CHUNKS = NQ // P
 COPY = mybir.ActivationFunctionType.Copy
-SPLIT = 288
-MOVES_ON_SYNC = 6
+SPLIT = 384
 
 
 def interleave(copy, grouped, planes):
@@ -61,12 +60,11 @@ def tile_attend_mlp_gelu_srt_kernel(tc, qT, k_words, k_scales, vT, us, offs, out
         nc.sync.dma_start(offsets[:], offs)
 
         scale_table = staged([P, T], U8, "scale_table", 6 * BUFFER)
-        nc.sync.dma_start(out=scale_table[0:32, :].bitcast(I32), in_=k_scales.rearrange("o f t -> (o f) t").bitcast(I32))
+        nc.sync.dma_start(out=scale_table[0:32, :].bitcast(I32), in_=k_scales.rearrange("o f t -> f o t").bitcast(I32))
         nc.vector.memset(scale_table[32:64, :].bitcast(I32), 0)
         nc.vector.memset(scale_table[64:128, :].bitcast(I32), 0)
-        scale_placed = [staged([P, N], U8, "scale_placed%d" % o, 10 * BUFFER + 4096 * o) for o in range(PASSES)]
-        for o in range(PASSES):
-            nc.vector.memset(scale_placed[o][:].bitcast(I32), 0)
+        scale_placed = sb.tile([P, PASSES * N], U8, name="scale_placed")
+        nc.vector.memset(scale_placed[:].bitcast(I32), 0)
 
         us_cols = sb.tile([P, PACK], F32, name="us_cols")
         nc.gpsimd.dma_start(out=us_cols[:], in_=us[0].rearrange("(p t) x -> p (t x)", t=PACK))
@@ -83,17 +81,13 @@ def tile_attend_mlp_gelu_srt_kernel(tc, qT, k_words, k_scales, vT, us, offs, out
         nc.vector.memset(warm[:, 0:1], 0.0)
         nc.scalar.activation(out=warm[:, 1:2], in_=warm[:, 0:1], func=GELU)
 
-        scale_picked = sb.tile([P, N], U8, name="scale_picked")
+        scale_picked = staged([P, N], U8, "scale_picked", 10 * BUFFER + 768)
         nc.vector.tensor_copy(scale_picked[:], scale_table[:].indirect(offsets[:]))
-        moves = [(o, quad) for o in range(PASSES) for quad in range(QUADS) if (o, quad) != (0, 0)]
-        for number, (o, quad) in enumerate(moves):
-            queue = nc.sync if number < MOVES_ON_SYNC else nc.gpsimd
-            row = 16 * o + 4 * quad
-            queue.dma_start(
-                out=scale_placed[o][32 * quad : 32 * quad + 4, :].bitcast(I32),
-                in_=scale_picked[row : row + 4, :].bitcast(I32),
+        for quad in range(QUADS):
+            nc.sync.dma_start(
+                out=scale_placed[32 * quad : 32 * quad + 4, :].bitcast(I32),
+                in_=scale_picked[8 * quad : 8 * quad + 8, :].bitcast(I32),
             )
-        nc.vector.tensor_copy(scale_placed[0][0:32, :].bitcast(I32), scale_picked[0:32, :].bitcast(I32))
         q_raw.append(staged([P, PACK, NQ], F32, "q_raw1", 6 * BUFFER))
         nc.sync.dma_start(out=q_raw[1][:], in_=q_rows[1])
 
@@ -118,12 +112,13 @@ def tile_attend_mlp_gelu_srt_kernel(tc, qT, k_words, k_scales, vT, us, offs, out
             grouped = [staged([P, HALF, PACK], BF16, "q_grouped%d_%d" % (h, o), work + 2048 * (2 * o + h)) for h in range(2)]
             interleave(nc.vector.tensor_copy, grouped[0][:], q_raw[o][:, :, 0:HALF])
             interleave(nc.scalar.copy, grouped[1][:], q_raw[o][:, :, HALF:NQ])
-            nc.vector.tensor_copy(
-                out=k_plane[o][:].rearrange("p (t m) -> p t m", t=PACK),
-                in_=scale_placed[o][:].rearrange("p (m t) -> p t m", t=PACK),
-            )
             for h in range(2):
-                codes = staged([P, HALF], U32, "q_codes%d_%d" % (h, o), 10 * BUFFER + 4096 * o + 1024 * ((h + o + 1) % 2))
+                if o == 0:
+                    nc.vector.tensor_copy(
+                        out=k_plane[h][:].rearrange("p (t m) -> p t m", t=PACK),
+                        in_=scale_placed[:, N * h : N * (h + 1)].rearrange("p (m t) -> p t m", t=PACK),
+                    )
+                codes = staged([P, HALF], U32, "q_codes%d_%d" % (h, o), 10 * BUFFER + 1024 * (2 * o + h))
                 q_mx[h, o] = quantize(nc, sb, grouped[h][:], "q%d_%d" % (h, o), codes)
             for c in range(CHUNKS):
                 cols = slice(P * (c % 2), P * (c % 2 + 1))
@@ -176,7 +171,7 @@ def tile_attend_mlp_gelu_srt_kernel(tc, qT, k_words, k_scales, vT, us, offs, out
 
         out_view = out[0].rearrange("(c p) e -> p c e", p=P)
 
-        def second_layer(e0, v_mx, chunks, copy, number, at):
+        def second_layer(e0, v_mx, chunks, copy, number, at, queue=nc.sync):
             width = v_mx[0].shape[1]
             res_acc = bank([P, len(chunks), width], "res_acc%d_%d" % (e0, chunks[0]), number)
             for place, c in enumerate(chunks):
@@ -192,11 +187,11 @@ def tile_attend_mlp_gelu_srt_kernel(tc, qT, k_words, k_scales, vT, us, offs, out
                 )
             res = staged([P, len(chunks), width], F32, "res%d_%d" % (e0, chunks[0]), at)
             copy(out=res[:], in_=res_acc[:])
-            nc.sync.dma_start(out=out_view[:, chunks[0] : chunks[-1] + 1, e0 : e0 + width], in_=res[:])
+            queue.dma_start(out=out_view[:, chunks[0] : chunks[-1] + 1, e0 : e0 + width], in_=res[:])
 
         every = list(range(CHUNKS))
         results = 8 * BUFFER
-        v_at = [9 * BUFFER, 9 * BUFFER + 1024, 3 * BUFFER + 4096, 9 * BUFFER + 2048]
+        v_at = [9 * BUFFER + 1024 * j for j in range(V_TILES)]
         v = [staged([P, P, PACK], BF16, "v%d" % j, v_at[j]) for j in range(V_TILES)]
         gather_on_vector(0, 0, N)
         for h in range(2):
@@ -209,13 +204,14 @@ def tile_attend_mlp_gelu_srt_kernel(tc, qT, k_words, k_scales, vT, us, offs, out
         turn_values(1, v[1][:], 5, nc.scalar.copy)
         second_layer(0, v0_mx, every, nc.scalar.copy, 0, results)
         v1_mx = quantize(nc, sb, v[1][:], "v1", staged([P, P], U32, "v1_codes", 2 * BUFFER))
+        turn_values(2, v[2][:], 6, nc.scalar.copy)
         gather_on_vector(3, 0, SPLIT)
         gather_on_scalar(3, SPLIT, N)
-        turn_values(2, v[2][:], 6, nc.scalar.copy)
+        v2_mx = quantize(nc, sb, v[2][:], "v2", staged([P, P], U32, "v2_codes", 3 * BUFFER + 4096))
         second_layer(P, v1_mx, every, nc.vector.tensor_copy, 1, 3 * BUFFER)
         turn_values(3, v[3][:], 7, nc.scalar.copy)
-        v2_mx = quantize(nc, sb, v[2][:], "v2")
         v3_mx = quantize(nc, sb, v[3][:], "v3")
         second_layer(2 * P, v2_mx, every, nc.scalar.copy, 2, results + 2048)
-        second_layer(3 * P, v3_mx, [0, 1], nc.vector.tensor_copy, 3, results + 4096)
-        second_layer(3 * P, v3_mx, [2, 3], nc.scalar.copy, 4, results + 5120)
+        for c in every:
+            copy, queue = [(nc.vector.tensor_copy, nc.sync), (nc.scalar.copy, nc.scalar)][c % 2]
+            second_layer(3 * P, v3_mx, [c], copy, [3, 4, 5, 0][c], results + 4096 + 512 * c, queue)

@@ -210,8 +210,9 @@ def tile_attend_mlp_gelu_srt_kernel(tc, qT, k_words, k_scales, vT, us, offs, out
         v2_mx = quantize(nc, sb, v[2][:], "v2", staged([P, P], U32, "v2_codes", 3 * BUFFER + 4096))
         second_layer(P, v1_mx, every, nc.vector.tensor_copy, 1, 3 * BUFFER)
         turn_values(3, v[3][:], 7, nc.scalar.copy)
+        second_layer(2 * P, v2_mx, every[:2], nc.vector.tensor_copy, 2, results + 2048)
+        second_layer(2 * P, v2_mx, every[2:], nc.scalar.copy, 6, results + 3072)
         v3_mx = quantize(nc, sb, v[3][:], "v3")
-        second_layer(2 * P, v2_mx, every, nc.scalar.copy, 2, results + 2048)
         for c in every:
             copy, queue = [(nc.vector.tensor_copy, nc.sync), (nc.scalar.copy, nc.scalar)][c % 2]
             second_layer(3 * P, v3_mx, [c], copy, [3, 4, 5, 0][c], results + 4096 + 512 * c, queue)

@@ -105,7 +105,7 @@ def tile_attend_mlp_gelu_srt_kernel(tc, qT, k_words, k_scales, vT, us, offs, out
             nc.sync.dma_start(out=v_table[j][:], in_=vT[P * j : P * (j + 1), :])
 
         work = 4 * BUFFER
-        acc = [bank([P, PACK, P], "acc%d" % c, c) for c in range(CHUNKS)]
+        acc = {(h, u): bank([P, 2, HALF], "acc%d_%d" % (h, u), 2 * h + u) for h in range(2) for u in range(2)}
         q_mx = {}
         k_plane = [sb.tile([P, N], U8, name="k_plane%d" % o, align_bytes=64) for o in range(PASSES)]
         for o in range(PASSES):
@@ -120,33 +120,31 @@ def tile_attend_mlp_gelu_srt_kernel(tc, qT, k_words, k_scales, vT, us, offs, out
                     )
                 codes = staged([P, HALF], U32, "q_codes%d_%d" % (h, o), 10 * BUFFER + 1024 * (2 * o + h))
                 q_mx[h, o] = quantize(nc, sb, grouped[h][:], "q%d_%d" % (h, o), codes)
-            for c in range(CHUNKS):
-                cols = slice(P * (c % 2), P * (c % 2 + 1))
+            for h in range(2):
                 for t in range(PACK):
                     at = (t * PASSES + o) * 2 * P
                     nc.tensor.matmul_mx(
-                        out=acc[c][:, t, :],
+                        out=acc[h, t // 2][:, t % 2, :],
                         lhsT=k_codes[:, at : at + 2 * P].bitcast(FP4X4),
                         lhsT_scale=k_plane[o][:, P * t : P * (t + 1)],
-                        rhs=q_mx[c // 2, o][0][:, cols].bitcast(FP8X4),
-                        rhs_scale=q_mx[c // 2, o][1][:, cols],
-                        start=(o == 0 and t == 0),
-                        stop=(o == PASSES - 1 and t == PACK - 1),
+                        rhs=q_mx[h, o][0][:].bitcast(FP8X4),
+                        rhs_scale=q_mx[h, o][1][:],
+                        start=(o == 0 and t % 2 == 0),
+                        stop=(o == PASSES - 1 and t % 2 == 1),
                     )
 
         late = 5 * BUFFER
         y = staged([P, NQ, PACK], BF16, "y", late)
-        acts = [staged([P, HALF, PACK], F32, "act%d" % h, 7 * BUFFER + 4096 * h) for h in range(2)]
-        for c in range(CHUNKS):
-            nc.scalar.activation(
-                out=acts[c // 2][:, P * (c % 2) : P * (c % 2 + 1), :], in_=acc[c][:].rearrange("p t q -> p q t"), func=GELU
-            )
+        acts = [staged([P, 2, HALF, 2], F32, "act%d" % h, 7 * BUFFER + 4096 * h) for h in range(2)]
+        for h in range(2):
+            for u in range(2):
+                nc.scalar.activation(out=acts[h][:, u], in_=acc[h, u][:].rearrange("p e q -> p q e"), func=GELU)
 
         def scale_rows(h):
             nc.vector.tensor_tensor(
-                out=y[:, HALF * h : HALF * (h + 1), :],
-                in0=acts[h][:],
-                in1=us_cols[:].unsqueeze(1).to_broadcast([P, HALF, PACK]),
+                out=y[:, HALF * h : HALF * (h + 1), :].rearrange("p q (u e) -> p q u e", u=2),
+                in0=acts[h][:].rearrange("p u q e -> p q u e"),
+                in1=us_cols[:].rearrange("p (u e) -> p u e", u=2).unsqueeze(1).to_broadcast([P, HALF, 2, 2]),
                 op=MULT,
             )
 

@@ -110,8 +110,14 @@ def tile_attend_mlp_gelu_srt_kernel(tc, qT, k_words, k_scales, vT, us, offs, out
         k_plane = [sb.tile([P, N], U8, name="k_plane%d" % o, align_bytes=64) for o in range(PASSES)]
         for o in range(PASSES):
             grouped = [staged([P, HALF, PACK], BF16, "q_grouped%d_%d" % (h, o), work + 2048 * (2 * o + h)) for h in range(2)]
-            interleave(nc.vector.tensor_copy, grouped[0][:], q_raw[o][:, :, 0:HALF])
-            interleave(nc.scalar.copy, grouped[1][:], q_raw[o][:, :, HALF:NQ])
+            if o == 0:
+                interleave(nc.vector.tensor_copy, grouped[0][:], q_raw[o][:, :, 0:HALF])
+                interleave(nc.scalar.copy, grouped[1][:], q_raw[o][:, :, HALF:NQ])
+            else:
+                for c in range(CHUNKS):
+                    copy = [nc.vector.tensor_copy, nc.scalar.copy][c % 2]
+                    rows = grouped[c // 2][:, P * (c % 2) : P * (c % 2 + 1), :]
+                    interleave(copy, rows, q_raw[o][:, :, P * c : P * (c + 1)])
             for h in range(2):
                 if o == 0:
                     nc.vector.tensor_copy(
@@ -208,9 +214,8 @@ def tile_attend_mlp_gelu_srt_kernel(tc, qT, k_words, k_scales, vT, us, offs, out
         v2_mx = quantize(nc, sb, v[2][:], "v2", staged([P, P], U32, "v2_codes", 3 * BUFFER + 4096))
         second_layer(P, v1_mx, every, nc.vector.tensor_copy, 1, 3 * BUFFER)
         turn_values(3, v[3][:], 7, nc.scalar.copy)
-        second_layer(2 * P, v2_mx, every[:2], nc.vector.tensor_copy, 2, results + 2048)
-        second_layer(2 * P, v2_mx, every[2:], nc.scalar.copy, 6, results + 3072)
         v3_mx = quantize(nc, sb, v[3][:], "v3")
+        second_layer(2 * P, v2_mx, every, nc.scalar.copy, 2, results + 2048)
         for c in every:
             copy, queue = [(nc.vector.tensor_copy, nc.sync), (nc.scalar.copy, nc.scalar)][c % 2]
             second_layer(3 * P, v3_mx, [c], copy, [3, 4, 5, 0][c], results + 4096 + 512 * c, queue)

@@ -27,7 +27,7 @@ HALF = NQ // 2
 BUFFER = 4 * T
 CHUNKS = NQ // P
 COPY = mybir.ActivationFunctionType.Copy
-SPLIT = 384
+SPLIT = 320
 
 
 def interleave(copy, grouped, planes):

@@ -31,7 +31,10 @@ SPLIT = 320
 
 
 def interleave(copy, grouped, planes):
-    copy(out=grouped, in_=planes.rearrange("p t w -> p w t"))
+    copy(
+        out=grouped.rearrange("p (c i) t -> p c t i", i=PACK),
+        in_=planes.rearrange("p t (c i) -> p c t i", i=PACK),
+    )
 
 
 def quantize(nc, pool, grouped, name, codes=None):

@@ -62,6 +62,9 @@ def tile_attend_mlp_gelu_srt_kernel(tc, qT, k_words, k_scales, vT, us, offs, out
         offsets = sb.tile([P, N // 16], U16, name="offsets")
         nc.sync.dma_start(offsets[:], offs)
 
+        us_row = sb.tile([P, N], F32, name="us_row")
+        nc.gpsimd.memset(us_row[:], 0.0)
+
         scale_table = staged([P, T], U8, "scale_table", 6 * BUFFER)
         nc.sync.dma_start(out=scale_table[0:32, :].bitcast(I32), in_=k_scales.rearrange("o f t -> f o t").bitcast(I32))
         nc.vector.memset(scale_table[32:64, :].bitcast(I32), 0)
@@ -69,13 +72,17 @@ def tile_attend_mlp_gelu_srt_kernel(tc, qT, k_words, k_scales, vT, us, offs, out
         scale_placed = sb.tile([P, PASSES * N], U8, name="scale_placed")
         nc.vector.memset(scale_placed[:].bitcast(I32), 0)
 
-        us_cols = sb.tile([P, PACK], F32, name="us_cols")
-        nc.gpsimd.dma_start(out=us_cols[:], in_=us[0].rearrange("(p t) x -> p (t x)", t=PACK))
-        ident = sb.tile([P, P], F32, name="ident")
-        make_identity(nc, ident[:])
-
         word_table = staged([P, T], I32, "word_table", BUFFER // 2)
         nc.sync.dma_start(out=word_table[:], in_=k_words[0].rearrange("g t b -> g (t b)").bitcast(I32))
+        nc.sync.dma_start(out=us_row[0:1, :], in_=us[0].rearrange("n x -> x n"))
+        ident = sb.tile([P, P], F32, name="ident")
+        make_identity(nc, ident[:])
+        us_turned = bank([P, PACK, P], "us_turned", 7)
+        for t in range(PACK):
+            nc.tensor.transpose(us_turned[:, t, :], us_row[:, t:N:PACK], ident[:])
+        us_cols = sb.tile([P, PACK], F32, name="us_cols")
+        nc.scalar.copy(out=us_cols[:], in_=us_turned[:, :, 0])
+
         q_rows = [qT[0, K_PASS * o : K_PASS * (o + 1), :].rearrange("(p t) w -> p t w", t=PACK) for o in range(PASSES)]
         q_raw = [sb.tile([P, PACK, NQ], F32, name="q_raw0")]
         nc.sync.dma_start(out=q_raw[0][:], in_=q_rows[0])

@@ -28,6 +28,7 @@ BUFFER = 4 * T
 CHUNKS = NQ // P
 COPY = mybir.ActivationFunctionType.Copy
 SPLIT = 320
+SHARE = 384
 
 
 def interleave(copy, grouped, planes):
@@ -205,7 +206,7 @@ def tile_attend_mlp_gelu_srt_kernel(tc, qT, k_words, k_scales, vT, us, offs, out
 
         every = list(range(CHUNKS))
         results = 8 * BUFFER
-        v_at = [9 * BUFFER + 1024 * j for j in range(V_TILES)]
+        v_at = [9 * BUFFER, 2 * BUFFER + 1024, 9 * BUFFER + 2048, 9 * BUFFER + 3072]
         v = [staged([P, P, PACK], BF16, "v%d" % j, v_at[j]) for j in range(V_TILES)]
         gather_on_vector(0, 0, N)
         for h in range(2):
@@ -214,9 +215,10 @@ def tile_attend_mlp_gelu_srt_kernel(tc, qT, k_words, k_scales, vT, us, offs, out
         gather_on_scalar(1, 0, N)
         v0_mx = quantize(nc, sb, v[0][:], "v0")
         y_mx = quantize(nc, sb, y[:], "y")
-        gather_on_vector(2, 0, N)
+        gather_on_vector(2, 0, SHARE)
+        gather_on_scalar(2, SHARE, N)
         turn_values(1, v[1][:], 5, nc.scalar.copy)
-        second_layer(0, v0_mx, every, nc.scalar.copy, 0, results)
+        second_layer(0, v0_mx, every, nc.scalar.copy, 0, 2 * BUFFER + 2048)
         v1_mx = quantize(nc, sb, v[1][:], "v1", staged([P, P], U32, "v1_codes", 2 * BUFFER))
         turn_values(2, v[2][:], 6, nc.scalar.copy)
         gather_on_vector(3, 0, SPLIT)

from contextlib import ExitStack

import concourse.mybir as mybir
from concourse.masks import make_identity

N, T, D, NQ, DV = 512, 2048, 1024, 512, 512
FLOPS = 2 * N * D * NQ + 2 * NQ * N * DV

F32 = mybir.dt.float32
BF16 = mybir.dt.bfloat16
I32 = mybir.dt.int32
U32 = mybir.dt.uint32
U16 = mybir.dt.uint16
U8 = mybir.dt.uint8
FP8X4 = mybir.dt.float8_e4m3fn_x4
FP4X4 = mybir.dt.float4_e2m1fn_x4
GELU = mybir.ActivationFunctionType.Gelu_apprx_tanh
MULT = mybir.AluOpType.mult

P = 128
PACK = 4
K_PASS = P * PACK
PASSES = D // K_PASS
QUADS = 4
V_TILES = DV // P
HALF = NQ // 2
BUFFER = 4 * T
CHUNKS = NQ // P
COPY = mybir.ActivationFunctionType.Copy
SPLIT = 320
SHARE = 384


def interleave(copy, grouped, planes):
    copy(
        out=grouped.rearrange("p (c i) t -> p c t i", i=PACK),
        in_=planes.rearrange("p t (c i) -> p c t i", i=PACK),
    )


def quantize(nc, pool, grouped, name, codes=None):
    width = grouped.shape[1]
    if codes is None:
        codes = pool.tile([P, width], U32, name=name + "_codes", align_bytes=64)
    scales = pool.tile([P, width], U8, name=name + "_scales", align_bytes=64)
    nc.vector.quantize_mx(out=codes[:].bitcast(FP8X4), scales=scales[:], in_=grouped.rearrange("p w t -> p (w t)"))
    return codes, scales


def tile_attend_mlp_gelu_srt_kernel(tc, qT, k_words, k_scales, vT, us, offs, out):
    nc = tc.nc
    with ExitStack() as ctx:
        sb = ctx.enter_context(tc.tile_pool(name="sb", bufs=1))
        staging = ctx.enter_context(tc.tile_pool(name="staging", bufs=1))
        ps = ctx.enter_context(tc.psum_pool(name="ps", bufs=1))

        def staged(shape, dtype, name, at):
            return staging.tile(shape, dtype, name=name, offset=at, align_bytes=64)

        def bank(shape, name, number):
            return ps.tile(shape, F32, name=name, offset=number * 2048)

        offsets = sb.tile([P, N // 16], U16, name="offsets")
        nc.sync.dma_start(offsets[:], offs)

        us_row = sb.tile([P, N], F32, name="us_row")
        nc.gpsimd.memset(us_row[:], 0.0)

        scale_table = staged([P, T], U8, "scale_table", 6 * BUFFER)
        nc.sync.dma_start(out=scale_table[0:32, :].bitcast(I32), in_=k_scales.rearrange("o f t -> f o t").bitcast(I32))
        nc.vector.memset(scale_table[32:64, :].bitcast(I32), 0)
        nc.vector.memset(scale_table[64:128, :].bitcast(I32), 0)
        scale_placed = sb.tile([P, PASSES * N], U8, name="scale_placed")
        nc.vector.memset(scale_placed[:].bitcast(I32), 0)

        word_table = staged([P, T], I32, "word_table", BUFFER // 2)
        nc.sync.dma_start(out=word_table[:], in_=k_words[0].rearrange("g t b -> g (t b)").bitcast(I32))
        nc.sync.dma_start(out=us_row[0:1, :], in_=us[0].rearrange("n x -> x n"))
        ident = sb.tile([P, P], F32, name="ident")
        make_identity(nc, ident[:])
        us_turned = bank([P, PACK, P], "us_turned", 7)
        for t in range(PACK):
            nc.tensor.transpose(us_turned[:, t, :], us_row[:, t:N:PACK], ident[:])
        us_cols = sb.tile([P, PACK], F32, name="us_cols")
        nc.scalar.copy(out=us_cols[:], in_=us_turned[:, :, 0])

        q_rows = [qT[0, K_PASS * o : K_PASS * (o + 1), :].rearrange("(p t) w -> p t w", t=PACK) for o in range(PASSES)]
        q_raw = [sb.tile([P, PACK, NQ], F32, name="q_raw0")]
        nc.sync.dma_start(out=q_raw[0][:], in_=q_rows[0])

        warm = sb.tile([P, 2], F32, name="warm")
        nc.vector.memset(warm[:, 0:1], 0.0)
        nc.scalar.activation(out=warm[:, 1:2], in_=warm[:, 0:1], func=GELU)

        scale_picked = staged([P, N], U8, "scale_picked", 10 * BUFFER + 768)
        nc.vector.tensor_copy(scale_picked[:], scale_table[:].indirect(offsets[:]))
        for quad in range(QUADS):
            nc.sync.dma_start(
                out=scale_placed[32 * quad : 32 * quad + 4, :].bitcast(I32),
                in_=scale_picked[8 * quad : 8 * quad + 8, :].bitcast(I32),
            )
        q_raw.append(staged([P, PACK, NQ], F32, "q_raw1", 6 * BUFFER))
        nc.sync.dma_start(out=q_raw[1][:], in_=q_rows[1])

        word_picked = staged([P, N], U32, "word_picked", 3 * BUFFER - 1024)
        nc.vector.tensor_copy(word_picked[:], word_table[:].bitcast(U32).indirect(offsets[:]))
        k_codes = sb.tile([P, PASSES * PACK * P * 2], U8, name="k_codes", align_bytes=64)
        nc.vector.tensor_copy(
            out=k_codes[:].bitcast(U16).rearrange("p (t o m) -> p t m o", t=PACK, o=PASSES),
            in_=word_picked[:].bitcast(U16).rearrange("p (m t o) -> p t m o", t=PACK, o=PASSES),
        )

        v_table = []
        for j in range(V_TILES):
            v_table.append(staged([P, T], F32, "v_table%d" % j, j * BUFFER))
            nc.sync.dma_start(out=v_table[j][:], in_=vT[P * j : P * (j + 1), :])

        work = 4 * BUFFER
        acc = {(h, u): bank([P, 2, HALF], "acc%d_%d" % (h, u), 2 * h + u) for h in range(2) for u in range(2)}
        q_mx = {}
        k_plane = [sb.tile([P, N], U8, name="k_plane%d" % o, align_bytes=64) for o in range(PASSES)]
        for o in range(PASSES):
            grouped = [staged([P, HALF, PACK], BF16, "q_grouped%d_%d" % (h, o), work + 2048 * (2 * o + h)) for h in range(2)]
            if o == 0:
                interleave(nc.vector.tensor_copy, grouped[0][:], q_raw[o][:, :, 0:HALF])
                interleave(nc.scalar.copy, grouped[1][:], q_raw[o][:, :, HALF:NQ])
            else:
                for c in range(CHUNKS):
                    copy = [nc.vector.tensor_copy, nc.scalar.copy][c % 2]
                    rows = grouped[c // 2][:, P * (c % 2) : P * (c % 2 + 1), :]
                    interleave(copy, rows, q_raw[o][:, :, P * c : P * (c + 1)])
            for h in range(2):
                if o == 0:
                    nc.vector.tensor_copy(
                        out=k_plane[h][:].rearrange("p (t m) -> p t m", t=PACK),
                        in_=scale_placed[:, N * h : N * (h + 1)].rearrange("p (m t) -> p t m", t=PACK),
                    )
                codes = staged([P, HALF], U32, "q_codes%d_%d" % (h, o), 10 * BUFFER + 1024 * (2 * o + h))
                q_mx[h, o] = quantize(nc, sb, grouped[h][:], "q%d_%d" % (h, o), codes)
            for h in range(2):
                for t in range(PACK):
                    at = (t * PASSES + o) * 2 * P
                    nc.tensor.matmul_mx(
                        out=acc[h, t // 2][:, t % 2, :],
                        lhsT=k_codes[:, at : at + 2 * P].bitcast(FP4X4),
                        lhsT_scale=k_plane[o][:, P * t : P * (t + 1)],
                        rhs=q_mx[h, o][0][:].bitcast(FP8X4),
                        rhs_scale=q_mx[h, o][1][:],
                        start=(o == 0 and t % 2 == 0),
                        stop=(o == PASSES - 1 and t % 2 == 1),
                    )

        late = 5 * BUFFER
        y = staged([P, NQ, PACK], BF16, "y", late)
        acts = [staged([P, 2, HALF, 2], F32, "act%d" % h, 7 * BUFFER + 4096 * h) for h in range(2)]
        for h in range(2):
            for u in range(2):
                nc.scalar.activation(out=acts[h][:, u], in_=acc[h, u][:].rearrange("p e q -> p q e"), func=GELU)

        def scale_rows(h):
            nc.vector.tensor_tensor(
                out=y[:, HALF * h : HALF * (h + 1), :].rearrange("p q (u e) -> p q u e", u=2),
                in0=acts[h][:].rearrange("p u q e -> p q u e"),
                in1=us_cols[:].rearrange("p (u e) -> p u e", u=2).unsqueeze(1).to_broadcast([P, HALF, 2, 2]),
                op=MULT,
            )

        picked_at = [work + 2048 * 3, 7 * BUFFER, 11 * BUFFER, 11 * BUFFER + 1024]
        picked = [staged([P, N], BF16, "v_picked%d" % j, picked_at[j]) for j in range(V_TILES)]

        def gather_on_vector(j, a, b):
            nc.vector.tensor_copy(picked[j][:, a:b], v_table[j][:].indirect(offsets[:, a // 16 : b // 16]))

        def gather_on_scalar(j, a, b):
            nc.scalar.activation(picked[j][:, a:b], v_table[j][:].indirect(offsets[:, a // 16 : b // 16]), COPY)

        def turn_values(j, grouped, number, copy):
            pairs = picked[j][:].bitcast(F32)
            turned = bank([P, 2, P], "turned%d" % j, number)
            for u in range(2):
                nc.tensor.transpose(turned[:, u, :], pairs[:, u : 2 * P : 2], ident[:])
            copy(
                out=grouped.rearrange("p e t -> p (e t)").bitcast(F32).rearrange("p (e u) -> p e u", u=2),
                in_=turned[:].rearrange("p u e -> p e u"),
            )

        out_view = out[0].rearrange("(c p) e -> p c e", p=P)

        def second_layer(e0, v_mx, chunks, copy, number, at, queue=nc.sync):
            width = v_mx[0].shape[1]
            res_acc = bank([P, len(chunks), width], "res_acc%d_%d" % (e0, chunks[0]), number)
            for place, c in enumerate(chunks):
                cols = slice(P * c, P * (c + 1))
                nc.tensor.matmul_mx(
                    out=res_acc[:, place, :],
                    lhsT=y_mx[0][:, cols].bitcast(FP8X4),
                    lhsT_scale=y_mx[1][:, cols],
                    rhs=v_mx[0][:].bitcast(FP8X4),
                    rhs_scale=v_mx[1][:],
                    start=True,
                    stop=True,
                )
            res = staged([P, len(chunks), width], F32, "res%d_%d" % (e0, chunks[0]), at)
            copy(out=res[:], in_=res_acc[:])
            queue.dma_start(out=out_view[:, chunks[0] : chunks[-1] + 1, e0 : e0 + width], in_=res[:])

        every = list(range(CHUNKS))
        results = 8 * BUFFER
        v_at = [9 * BUFFER, 2 * BUFFER + 1024, 9 * BUFFER + 2048, 9 * BUFFER + 3072]
        v = [staged([P, P, PACK], BF16, "v%d" % j, v_at[j]) for j in range(V_TILES)]
        gather_on_vector(0, 0, N)
        for h in range(2):
            scale_rows(h)
        turn_values(0, v[0][:], 4, nc.scalar.copy)
        gather_on_scalar(1, 0, N)
        v0_mx = quantize(nc, sb, v[0][:], "v0")
        y_mx = quantize(nc, sb, y[:], "y")
        gather_on_vector(2, 0, SHARE)
        gather_on_scalar(2, SHARE, N)
        turn_values(1, v[1][:], 5, nc.scalar.copy)
        second_layer(0, v0_mx, every, nc.scalar.copy, 0, 2 * BUFFER + 2048)
        v1_mx = quantize(nc, sb, v[1][:], "v1", staged([P, P], U32, "v1_codes", 2 * BUFFER))
        turn_values(2, v[2][:], 6, nc.scalar.copy)
        gather_on_vector(3, 0, SPLIT)
        gather_on_scalar(3, SPLIT, N)
        v2_mx = quantize(nc, sb, v[2][:], "v2", staged([P, P], U32, "v2_codes", 3 * BUFFER + 4096))
        second_layer(P, v1_mx, every, nc.vector.tensor_copy, 1, 3 * BUFFER)
        turn_values(3, v[3][:], 7, nc.scalar.copy)
        v3_mx = quantize(nc, sb, v[3][:], "v3")
        second_layer(2 * P, v2_mx, every, nc.scalar.copy, 2, results + 2048)
        for c in every:
            copy, queue = [(nc.vector.tensor_copy, nc.sync), (nc.scalar.copy, nc.scalar)][c % 2]
            second_layer(3 * P, v3_mx, [c], copy, [3, 4, 5, 0][c], results + 4096 + 512 * c, queue)
